import numpy as np
import ml_dtypes


def mxq(x, axis, fmt="e4m3"):
    dtype, down = {"e4m3": (ml_dtypes.float8_e4m3fn, 7), "e5m2": (ml_dtypes.float8_e5m2, 14)}[fmt]
    v = np.moveaxis(np.asarray(x, np.float32).astype(ml_dtypes.bfloat16).astype(np.float64), axis, -1)
    blocks = v.reshape(v.shape[:-1] + (-1, 32))
    amax = np.abs(blocks).max(-1, keepdims=True)
    byte = np.maximum(np.where(amax > 0, np.frexp(amax)[1] - 1 + 127, 0) - down, 1)
    scale = np.exp2(byte - 127.0)
    codes = (blocks / scale).astype(np.float32).astype(dtype).astype(np.float64)
    return np.moveaxis((codes * scale).reshape(v.shape), -1, axis)


WIDE = False


def mx_kscale(k):
    if not WIDE:
        return np.ones(k)
    levels = np.array([10, -10, 5, -5, 0])
    if k % 512:
        return np.exp2(np.random.permutation(np.resize(levels, k // 32))).repeat(32)
    a = np.empty((k // 512, 16))
    for p in range(k // 512):
        a[p, :8] = np.random.permutation(np.resize(levels, 8))
        for g in range(8):
            far = levels[np.abs(levels - a[p, g]) >= 10]
            a[p, g + 8] = far[np.random.randint(len(far))]
    return np.exp2(a.ravel()).repeat(32)


def f64(x):
    return np.asarray(x).astype(np.float64)


def striped(idx):
    return np.tile(idx.reshape(-1, 16).T, (8, 1)).astype(np.uint16)


def unstriped(offs):
    return offs[:16].T.reshape(-1).astype(np.int64)


def pack_weight(w):
    k, n = w.shape
    w = f64(np.asarray(w, np.float32).astype(ml_dtypes.bfloat16)).reshape(k // 32, 32, n)
    amax = np.abs(w).max(1)
    byte = np.clip(np.where(amax > 0, np.frexp(amax)[1] - 1 + 127 - 7, 1), 1, 254)
    scaled = (w * np.exp2(127.0 - byte)[:, None, :]).reshape(k, n).astype(np.float32)
    words = np.ascontiguousarray(scaled.reshape(k // 512, 128, 4, n).transpose(0, 1, 3, 2)).astype(ml_dtypes.float8_e4m3fn).view(np.uint8)
    return words, np.ascontiguousarray(byte.astype(np.uint8).reshape(k // 512, 16, n))


def unpack_weight(words, scales):
    g, p, n, _ = words.shape
    vals = np.ascontiguousarray(words).view(ml_dtypes.float8_e4m3fn).astype(np.float64) * np.repeat(np.exp2(scales.astype(np.float64) - 127.0), 8, axis=1)[..., None]
    return vals.transpose(0, 1, 3, 2).reshape(g * 512, n)


def gelu(v):
    return 0.5 * v * (1.0 + np.tanh(np.sqrt(2.0 / np.pi) * (v + 0.044715 * v**3)))


K, T, S, H, N = 1024, 1024, 512, 512, 256
P = 2 ** 7


def setup_inputs():
    n = np.random.standard_normal
    s = mx_kscale(K)[:, None]
    u = mx_kscale(H)
    packed_w2 = pack_weight(n((H, N)) / np.sqrt(H) / u[:, None])
    return {
        "xT": (n((K, T)) * s).astype(np.float32),
        "w1": (n((K, H)) / np.sqrt(K) / s * u).astype(np.float32),
        "w2_words": packed_w2[0],
        "w2_scales": packed_w2[1],
        "lam": np.tile(np.random.uniform(0.1, 0.9, S), (P, 1)).astype(np.float32),
        "mu": np.tile(np.random.uniform(0.1, 0.9, S), (P, 1)).astype(np.float32),
        "offs": striped(np.random.permutation(T)[:S]),
        "pos1": striped(np.random.permutation(S)),
    }


def reference(xT, w1, w2_words, w2_scales, lam, mu, offs, pos1):
    xq = mxq(f64(xT)[:, unstriped(offs)], 0, "e4m3")
    h = gelu(mxq(f64(w1), 0, "e4m3").T @ xq)
    z = h * f64(lam)[:1] + h[:, unstriped(pos1)] * f64(mu)[:1]
    return unpack_weight(w2_words, w2_scales).T @ mxq(z, 0, "e4m3")

@@ -1,0 +1,200 @@
+from contextlib import ExitStack
+
+import concourse.mybir as mybir
+
+K, T, S, H, N = 1024, 1024, 512, 512, 256
+FLOPS = 2 * K * H * S + 2 * H * N * S
+
+F32 = mybir.dt.float32
+BF16 = mybir.dt.bfloat16
+I32 = mybir.dt.int32
+U32 = mybir.dt.uint32
+U16 = mybir.dt.uint16
+U8 = mybir.dt.uint8
+FP8X4 = mybir.dt.float8_e4m3fn_x4
+COPY = mybir.ActivationFunctionType.Copy
+GELU = mybir.ActivationFunctionType.Gelu_apprx_tanh
+MULT = mybir.AluOpType.mult
+ADD = mybir.AluOpType.add
+
+P = 128
+PACK = 4
+K_PASS = P * PACK
+PASSES = K // K_PASS
+X_CHUNKS = ((0, 0, 512), (0, 512, 1024), (1, 0, 512), (1, 512, 768), (1, 768, 1024))
+X_SCALAR_SHARE = (384, 384, 320, 96, 96)
+W_CHUNK = 256
+PIECE = 128
+H_COLS = S + 16
+
+
+def tile_picked_mixup_gelu_e_kernel(
+    tc, xT, w1, w2_words, w2_scales, lam, mu, offs, pos1, out
+):
+    nc = tc.nc
+
+    def on_vector(dst, src):
+        nc.vector.tensor_copy(out=dst, in_=src)
+
+    def on_scalar(dst, src):
+        nc.scalar.activation(out=dst, in_=src, func=COPY)
+
+    with ExitStack() as ctx:
+        keep = ctx.enter_context(tc.tile_pool(name="keep", bufs=1))
+        psum = ctx.enter_context(tc.psum_pool(name="psum", bufs=1))
+
+        offs_sb = keep.tile([P, S // 16], U16, name="offs_sb")
+        pos_sb = keep.tile([P, S // 16], U16, name="pos_sb")
+
+        x_scales = keep.tile([P, T], U8, name="x_scales", align_bytes=64)
+        w2_scale_sb = keep.tile([P, N], U8, name="w2_scale_sb", align_bytes=64)
+        nc.gpsimd.memset(x_scales[:], 0)
+        nc.gpsimd.memset(w2_scale_sb[:], 0)
+
+        warm = keep.tile([P, 8], F32, name="warm")
+        nc.vector.memset(warm[:], 0.0)
+        nc.scalar.activation(out=warm[:], in_=warm[:], func=GELU)
+
+        x_raw = []
+        for n, (g, a, b) in enumerate(X_CHUNKS):
+            x_raw.append(keep.tile([P, PACK, b - a], F32, name=f"x_raw{n}"))
+            rows = xT[g * K_PASS : (g + 1) * K_PASS, a:b]
+            nc.sync.dma_start(out=x_raw[n][:], in_=rows.rearrange("(p j) c -> p j c", j=PACK))
+            if n == 0:
+                nc.sync.dma_start(offs_sb[:], offs)
+        w_raw = {}
+        for g in range(PASSES):
+            for c in range(H // W_CHUNK):
+                w_raw[g, c] = keep.tile([P, PACK, W_CHUNK], F32, name=f"w_raw{g}{c}")
+                rows = w1[g * K_PASS : (g + 1) * K_PASS, c * W_CHUNK : (c + 1) * W_CHUNK]
+                nc.sync.dma_start(out=w_raw[g, c][:], in_=rows.rearrange("(p j) c -> p j c", j=PACK))
+        nc.sync.dma_start(pos_sb[:], pos1)
+        mu_sb = keep.tile([P, S], F32, name="mu_sb")
+        lam_sb = keep.tile([P, S], F32, name="lam_sb")
+        nc.sync.dma_start(out=mu_sb[:], in_=mu)
+        nc.sync.dma_start(out=lam_sb[:], in_=lam)
+        w2_codes = keep.tile([P, N], U32, name="w2_codes", align_bytes=64)
+        nc.sync.dma_start(
+            out=w2_codes[:].bitcast(I32), in_=w2_words[0].rearrange("p n t -> p (n t)").bitcast(I32)
+        )
+        for q in range(4):
+            nc.sync.dma_start(
+                out=w2_scale_sb[32 * q : 32 * q + 4, :].bitcast(I32),
+                in_=w2_scales[0, 4 * q : 4 * q + 4, :].bitcast(I32),
+            )
+
+        x_words = [keep.tile([P, T], U32, name=f"x_words{g}", align_bytes=64) for g in range(PASSES)]
+        picked_words = [keep.tile([P, S], U32, name=f"picked_words{g}", align_bytes=64) for g in range(PASSES)]
+        picked_scales = keep.tile([P, S], U8, name="picked_scales", align_bytes=64)
+        for n, (g, c0, c1) in enumerate(X_CHUNKS):
+            x_bf = keep.tile([P, c1 - c0, PACK], BF16, name=f"x_bf{n}", align_bytes=64)
+            split = X_SCALAR_SHARE[n]
+            for move, a, b in ((on_scalar, 0, split), (on_vector, split, c1 - c0)):
+                move(
+                    x_bf[:, a:b, :].rearrange("p (c i) j -> p c j i", i=4),
+                    x_raw[n][:, :, a:b].rearrange("p j (c i) -> p c j i", i=4),
+                )
+            nc.vector.quantize_mx(
+                out=x_words[g][:, c0:c1].bitcast(FP8X4),
+                scales=x_scales[4 * g :, c0:c1],
+                in_=x_bf[:].rearrange("p c j -> p (c j)"),
+            )
+            if c1 == T:
+                nc.vector.tensor_copy(out=picked_words[g][:], in_=x_words[g][:].indirect(offs_sb[:]))
+        nc.vector.tensor_copy(out=picked_scales[:], in_=x_scales[:].indirect(offs_sb[:]))
+
+        w_codes = [keep.tile([P, H], U32, name=f"w_codes{g}", align_bytes=64) for g in range(PASSES)]
+        w_scales = keep.tile([P, H], U8, name="w_scales", align_bytes=64)
+        w_scales_early = keep.tile([P, H // 2], U8, name="w_scales_early", align_bytes=64)
+
+        def w_plane(g, cols):
+            if g == 0 and cols.stop <= H // 2:
+                return w_scales_early[:, cols]
+            return w_scales[4 * g :, cols]
+
+        m_chunk = W_CHUNK // PACK
+        for g in range(PASSES):
+            w_bf = keep.tile([P, PACK, P, PACK], BF16, name=f"w_bf{g}", align_bytes=64)
+            for c in range(H // W_CHUNK):
+                last = (g, c) == (PASSES - 1, H // W_CHUNK - 1)
+                shares = ((on_scalar, 0, 20), (on_vector, 20, m_chunk)) if last else ((on_scalar, 0, m_chunk),)
+                for move, a, b in shares:
+                    move(
+                        w_bf[:, :, c * m_chunk + a : c * m_chunk + b, :].rearrange("p t m j -> p m j t"),
+                        w_raw[g, c][:, :, PACK * a : PACK * b].rearrange("p j (m t) -> p m j t", t=PACK),
+                    )
+            step = 2 if g == 0 else 1
+            for t in range(0, PACK, step):
+                cols = slice(t * P, (t + step) * P)
+                nc.vector.quantize_mx(
+                    out=w_codes[g][:, cols].bitcast(FP8X4),
+                    scales=w_plane(g, cols),
+                    in_=w_bf[:, t : t + step, :, :].rearrange("p t m j -> p (t m j)"),
+                )
+
+        h = []
+        for t in range(PACK):
+            u = psum.tile([P, S], F32, name=f"u{t}")
+            cols = slice(t * P, (t + 1) * P)
+            for g in range(PASSES):
+                nc.tensor.matmul_mx(
+                    out=u[:],
+                    lhsT=w_codes[g][:, cols].bitcast(FP8X4),
+                    lhsT_scale=w_plane(g, cols),
+                    rhs=picked_words[g][:].bitcast(FP8X4),
+                    rhs_scale=picked_scales[4 * g :, :],
+                    start=(g == 0),
+                    stop=(g == PASSES - 1),
+                )
+            h_t = keep.tile([P, H_COLS], F32, name=f"h{t}")
+            nc.gpsimd.memset(h_t[:, S:], 0.0)
+            nc.scalar.activation(out=h_t[:, :S], in_=u[:], func=GELU)
+            h.append(h_t)
+
+        out_view = out.rearrange("(b p) j -> p b j", p=P)
+        partner = keep.tile([P, PACK, S], F32, name="partner")
+        own = keep.tile([P, PACK, S], F32, name="own")
+        for t in range(PACK):
+            nc.vector.tensor_tensor(partner[:, t, :], h[t][:].indirect(pos_sb[:]), mu_sb[:], MULT)
+            nc.vector.tensor_tensor(own[:, t, :], h[t][:, :S], lam_sb[:], MULT)
+
+        pieces = S // PIECE
+        z_bf = [keep.tile([P, PIECE, PACK], BF16, name=f"z_bf{n}", align_bytes=64) for n in range(pieces)]
+
+        def mix(n):
+            cols = slice(n * PIECE, (n + 1) * PIECE)
+            nc.vector.tensor_tensor(
+                z_bf[n][:].rearrange("p (c i) t -> p c t i", i=4),
+                own[:, :, cols].rearrange("p t (c i) -> p c t i", i=4),
+                partner[:, :, cols].rearrange("p t (c i) -> p c t i", i=4),
+                ADD,
+            )
+
+        def second_product(n):
+            cols = slice(n * PIECE, (n + 1) * PIECE)
+            z_codes = keep.tile([P, PIECE], U32, name=f"z_codes{n}", align_bytes=64)
+            z_scales = keep.tile([P, PIECE], U8, name=f"z_scales{n}", align_bytes=64)
+            nc.vector.quantize_mx(
+                out=z_codes[:].bitcast(FP8X4), scales=z_scales[:], in_=z_bf[n][:].rearrange("p c t -> p (c t)")
+            )
+            y = psum.tile([P, N // P, PIECE], F32, name=f"y{n}")
+            for b in range(N // P):
+                rows = slice(b * P, (b + 1) * P)
+                nc.tensor.matmul_mx(
+                    out=y[:, b, :],
+                    lhsT=w2_codes[:, rows].bitcast(FP8X4),
+                    lhsT_scale=w2_scale_sb[:, rows],
+                    rhs=z_codes[:].bitcast(FP8X4),
+                    rhs_scale=z_scales[:],
+                    start=True,
+                    stop=True,
+                )
+            y_sb = keep.tile([P, N // P, PIECE], F32, name=f"y_sb{n}")
+            nc.scalar.copy(out=y_sb[:], in_=y[:])
+            nc.sync.dma_start(out=out_view[:, :, cols], in_=y_sb[:])
+
+        for n in range(pieces + 1):
+            if n < pieces:
+                mix(n)
+            if n > 0:
+                second_product(n - 1)

@@ -1,6 +1,7 @@
 from contextlib import ExitStack
 
 import concourse.mybir as mybir
+from concourse.masks import make_identity
 
 K, T, S, H, N = 1024, 1024, 512, 512, 256
 FLOPS = 2 * K * H * S + 2 * H * N * S
@@ -22,7 +23,7 @@ PACK = 4
 K_PASS = P * PACK
 PASSES = K // K_PASS
 X_CHUNKS = ((0, 0, 512), (0, 512, 1024), (1, 0, 512), (1, 512, 768), (1, 768, 1024))
-X_SCALAR_SHARE = (384, 384, 320, 96, 96)
+X_SCALAR_SHARE = (256, 256, 256, 96, 96)
 W_CHUNK = 256
 PIECE = 128
 H_COLS = S + 16
@@ -51,6 +52,9 @@ def tile_picked_mixup_gelu_e_kernel(
         nc.gpsimd.memset(x_scales[:], 0)
         nc.gpsimd.memset(w2_scale_sb[:], 0)
 
+        ident = keep.tile([P, P], F32, name="ident")
+        make_identity(nc, ident[:])
+
         warm = keep.tile([P, 8], F32, name="warm")
         nc.vector.memset(warm[:], 0.0)
         nc.scalar.activation(out=warm[:], in_=warm[:], func=GELU)
@@ -70,9 +74,9 @@ def tile_picked_mixup_gelu_e_kernel(
                 nc.sync.dma_start(out=w_raw[g, c][:], in_=rows.rearrange("(p j) c -> p j c", j=PACK))
         nc.sync.dma_start(pos_sb[:], pos1)
         mu_sb = keep.tile([P, S], F32, name="mu_sb")
-        lam_sb = keep.tile([P, S], F32, name="lam_sb")
+        lam_rows = keep.tile([P, P], F32, name="lam_rows")
         nc.sync.dma_start(out=mu_sb[:], in_=mu)
-        nc.sync.dma_start(out=lam_sb[:], in_=lam)
+        nc.sync.dma_start(out=lam_rows[:], in_=lam.rearrange("a (n j) -> (a n) j", j=P)[:P, :])
         w2_codes = keep.tile([P, N], U32, name="w2_codes", align_bytes=64)
         nc.sync.dma_start(
             out=w2_codes[:].bitcast(I32), in_=w2_words[0].rearrange("p n t -> p (n t)").bitcast(I32)
@@ -105,10 +109,10 @@ def tile_picked_mixup_gelu_e_kernel(
 
         w_codes = [keep.tile([P, H], U32, name=f"w_codes{g}", align_bytes=64) for g in range(PASSES)]
         w_scales = keep.tile([P, H], U8, name="w_scales", align_bytes=64)
-        w_scales_early = keep.tile([P, H // 2], U8, name="w_scales_early", align_bytes=64)
+        w_scales_early = keep.tile([P, P], U8, name="w_scales_early", align_bytes=64)
 
         def w_plane(g, cols):
-            if g == 0 and cols.stop <= H // 2:
+            if g == 0 and cols.stop <= P:
                 return w_scales_early[:, cols]
             return w_scales[4 * g :, cols]
 
@@ -117,14 +121,13 @@ def tile_picked_mixup_gelu_e_kernel(
             w_bf = keep.tile([P, PACK, P, PACK], BF16, name=f"w_bf{g}", align_bytes=64)
             for c in range(H // W_CHUNK):
                 last = (g, c) == (PASSES - 1, H // W_CHUNK - 1)
-                shares = ((on_scalar, 0, 20), (on_vector, 20, m_chunk)) if last else ((on_scalar, 0, m_chunk),)
+                shares = ((on_scalar, 0, 24), (on_vector, 24, m_chunk)) if last else ((on_scalar, 0, m_chunk),)
                 for move, a, b in shares:
                     move(
                         w_bf[:, :, c * m_chunk + a : c * m_chunk + b, :].rearrange("p t m j -> p m j t"),
                         w_raw[g, c][:, :, PACK * a : PACK * b].rearrange("p j (m t) -> p m j t", t=PACK),
                     )
-            step = 2 if g == 0 else 1
-            for t in range(0, PACK, step):
+            for t, step in ((0, 1), (1, 1), (2, 2)):
                 cols = slice(t * P, (t + step) * P)
                 nc.vector.quantize_mx(
                     out=w_codes[g][:, cols].bitcast(FP8X4),
@@ -134,38 +137,61 @@ def tile_picked_mixup_gelu_e_kernel(
 
         h = []
         for t in range(PACK):
-            u = psum.tile([P, S], F32, name=f"u{t}")
             cols = slice(t * P, (t + 1) * P)
-            for g in range(PASSES):
-                nc.tensor.matmul_mx(
-                    out=u[:],
-                    lhsT=w_codes[g][:, cols].bitcast(FP8X4),
-                    lhsT_scale=w_plane(g, cols),
-                    rhs=picked_words[g][:].bitcast(FP8X4),
-                    rhs_scale=picked_scales[4 * g :, :],
-                    start=(g == 0),
-                    stop=(g == PASSES - 1),
-                )
             h_t = keep.tile([P, H_COLS], F32, name=f"h{t}")
             nc.gpsimd.memset(h_t[:, S:], 0.0)
-            nc.scalar.activation(out=h_t[:, :S], in_=u[:], func=GELU)
+            parts = (("a0", 0, S // 2), ("b0", S // 2, S)) if t == 0 else ((f"a{t}", 0, S),)
+            for tag, a, b in parts:
+                u = psum.tile([P, b - a], F32, name=f"u{t}{tag}", tag=tag)
+                for g in range(PASSES):
+                    nc.tensor.matmul_mx(
+                        out=u[:],
+                        lhsT=w_codes[g][:, cols].bitcast(FP8X4),
+                        lhsT_scale=w_plane(g, cols),
+                        rhs=picked_words[g][:, a:b].bitcast(FP8X4),
+                        rhs_scale=picked_scales[4 * g :, a:b],
+                        start=(g == 0),
+                        stop=(g == PASSES - 1),
+                    )
+                nc.scalar.activation(out=h_t[:, a:b], in_=u[:], func=GELU)
             h.append(h_t)
 
         out_view = out.rearrange("(b p) j -> p b j", p=P)
         partner = keep.tile([P, PACK, S], F32, name="partner")
-        own = keep.tile([P, PACK, S], F32, name="own")
         for t in range(PACK):
             nc.vector.tensor_tensor(partner[:, t, :], h[t][:].indirect(pos_sb[:]), mu_sb[:], MULT)
-            nc.vector.tensor_tensor(own[:, t, :], h[t][:, :S], lam_sb[:], MULT)
 
         pieces = S // PIECE
+        lam_turned = psum.tile([P, P], F32, name="lam_turned", tag="b3")
+        nc.tensor.transpose(lam_turned[:], lam_rows[:], ident[:])
+        lam_col = keep.tile([P, pieces], F32, name="lam_col")
+        nc.scalar.copy(out=lam_col[:], in_=lam_turned[:, :pieces])
+
+        own = []
+        scaled = []
+
+        def turn_back(n):
+            own.append(psum.tile([P, PACK, PIECE], F32, name=f"own{n}", tag=f"a{n}"))
+            for t in range(PACK):
+                nc.tensor.transpose(own[n][:, t, :], scaled[n][:, t, :], ident[:])
+
+        for n in range(pieces):
+            turned = psum.tile([P, PACK, P], F32, name=f"turned{n}", tag=f"b{n}")
+            for t in range(PACK):
+                nc.tensor.transpose(turned[:, t, :], h[t][:, n * PIECE : (n + 1) * PIECE], ident[:])
+            scaled.append(keep.tile([P, PACK, P], F32, name=f"scaled{n}"))
+            nc.scalar.activation(out=scaled[n][:], in_=turned[:], func=COPY, scale=lam_col[:, n : n + 1])
+            if n > 0:
+                turn_back(n - 1)
+        turn_back(pieces - 1)
+
         z_bf = [keep.tile([P, PIECE, PACK], BF16, name=f"z_bf{n}", align_bytes=64) for n in range(pieces)]
 
         def mix(n):
             cols = slice(n * PIECE, (n + 1) * PIECE)
             nc.vector.tensor_tensor(
                 z_bf[n][:].rearrange("p (c i) t -> p c t i", i=4),
-                own[:, :, cols].rearrange("p t (c i) -> p c t i", i=4),
+                own[n][:].rearrange("p t (c i) -> p c t i", i=4),
                 partner[:, :, cols].rearrange("p t (c i) -> p c t i", i=4),
                 ADD,
             )
@@ -177,7 +203,7 @@ def tile_picked_mixup_gelu_e_kernel(
             nc.vector.quantize_mx(
                 out=z_codes[:].bitcast(FP8X4), scales=z_scales[:], in_=z_bf[n][:].rearrange("p c t -> p (c t)")
             )
-            y = psum.tile([P, N // P, PIECE], F32, name=f"y{n}")
+            y = psum.tile([P, N // P, PIECE], F32, name=f"y{n}", tag=f"b{n}")
             for b in range(N // P):
                 rows = slice(b * P, (b + 1) * P)
                 nc.tensor.matmul_mx(

@@ -23,8 +23,9 @@ PACK = 4
 K_PASS = P * PACK
 PASSES = K // K_PASS
 X_CHUNKS = ((0, 0, 512), (0, 512, 1024), (1, 0, 512), (1, 512, 768), (1, 768, 1024))
-X_SCALAR_SHARE = (256, 256, 256, 96, 96)
-W_CHUNK = 256
+X_SCALAR_SHARE = (256, 160, 256, 192, 96)
+W_CHUNKS = ((0, 0, 256), (0, 256, 512), (1, 0, 256), (1, 256, 384), (1, 384, 512))
+W_SCALAR_SHARE = (256, 256, 256, 0, 48)
 PIECE = 128
 H_COLS = S + 16
 
@@ -66,17 +67,18 @@ def tile_picked_mixup_gelu_e_kernel(
             nc.sync.dma_start(out=x_raw[n][:], in_=rows.rearrange("(p j) c -> p j c", j=PACK))
             if n == 0:
                 nc.sync.dma_start(offs_sb[:], offs)
-        w_raw = {}
-        for g in range(PASSES):
-            for c in range(H // W_CHUNK):
-                w_raw[g, c] = keep.tile([P, PACK, W_CHUNK], F32, name=f"w_raw{g}{c}")
-                rows = w1[g * K_PASS : (g + 1) * K_PASS, c * W_CHUNK : (c + 1) * W_CHUNK]
-                nc.sync.dma_start(out=w_raw[g, c][:], in_=rows.rearrange("(p j) c -> p j c", j=PACK))
+        w_raw = []
+        for n, (g, a, b) in enumerate(W_CHUNKS):
+            w_raw.append(keep.tile([P, PACK, b - a], F32, name=f"w_raw{n}"))
+            rows = w1[g * K_PASS : (g + 1) * K_PASS, a:b]
+            nc.sync.dma_start(out=w_raw[n][:], in_=rows.rearrange("(p j) c -> p j c", j=PACK))
         nc.sync.dma_start(pos_sb[:], pos1)
         mu_sb = keep.tile([P, S], F32, name="mu_sb")
         lam_rows = keep.tile([P, P], F32, name="lam_rows")
         nc.sync.dma_start(out=mu_sb[:], in_=mu)
         nc.sync.dma_start(out=lam_rows[:], in_=lam.rearrange("a (n j) -> (a n) j", j=P)[:P, :])
+        lam_first = keep.tile([P, PIECE], F32, name="lam_first")
+        nc.sync.dma_start(out=lam_first[:], in_=lam[:, :PIECE])
         w2_codes = keep.tile([P, N], U32, name="w2_codes", align_bytes=64)
         nc.sync.dma_start(
             out=w2_codes[:].bitcast(I32), in_=w2_words[0].rearrange("p n t -> p (n t)").bitcast(I32)
@@ -116,24 +118,22 @@ def tile_picked_mixup_gelu_e_kernel(
                 return w_scales_early[:, cols]
             return w_scales[4 * g :, cols]
 
-        m_chunk = W_CHUNK // PACK
-        for g in range(PASSES):
-            w_bf = keep.tile([P, PACK, P, PACK], BF16, name=f"w_bf{g}", align_bytes=64)
-            for c in range(H // W_CHUNK):
-                last = (g, c) == (PASSES - 1, H // W_CHUNK - 1)
-                shares = ((on_scalar, 0, 24), (on_vector, 24, m_chunk)) if last else ((on_scalar, 0, m_chunk),)
-                for move, a, b in shares:
+        w_bf = [keep.tile([P, PACK, P, PACK], BF16, name=f"w_bf{g}", align_bytes=64) for g in range(PASSES)]
+        for n, (g, a, b) in enumerate(W_CHUNKS):
+            split = W_SCALAR_SHARE[n]
+            for move, c0, c1 in ((on_scalar, 0, split), (on_vector, split, b - a)):
+                if c1 > c0:
                     move(
-                        w_bf[:, :, c * m_chunk + a : c * m_chunk + b, :].rearrange("p t m j -> p m j t"),
-                        w_raw[g, c][:, :, PACK * a : PACK * b].rearrange("p j (m t) -> p m j t", t=PACK),
+                        w_bf[g][:, :, (a + c0) // PACK : (a + c1) // PACK, :].rearrange("p t m j -> p m j t"),
+                        w_raw[n][:, :, c0:c1].rearrange("p j (m t) -> p m j t", t=PACK),
                     )
-            for t, step in ((0, 1), (1, 1), (2, 2)):
-                cols = slice(t * P, (t + step) * P)
-                nc.vector.quantize_mx(
-                    out=w_codes[g][:, cols].bitcast(FP8X4),
-                    scales=w_plane(g, cols),
-                    in_=w_bf[:, t : t + step, :, :].rearrange("p t m j -> p (t m j)"),
-                )
+        for g, t0, t1 in ((0, 0, 1), (1, 0, 1), (1, 1, 2), (0, 1, 2), (1, 2, 4), (0, 2, 4)):
+            cols = slice(t0 * P, t1 * P)
+            nc.vector.quantize_mx(
+                out=w_codes[g][:, cols].bitcast(FP8X4),
+                scales=w_plane(g, cols),
+                in_=w_bf[g][:, t0:t1, :, :].rearrange("p t m j -> p (t m j)"),
+            )
 
         h = []
         for t in range(PACK):
@@ -158,8 +158,10 @@ def tile_picked_mixup_gelu_e_kernel(
 
         out_view = out.rearrange("(b p) j -> p b j", p=P)
         partner = keep.tile([P, PACK, S], F32, name="partner")
+        own_first = keep.tile([P, PACK, PIECE], F32, name="own_first")
         for t in range(PACK):
             nc.vector.tensor_tensor(partner[:, t, :], h[t][:].indirect(pos_sb[:]), mu_sb[:], MULT)
+            nc.vector.tensor_tensor(own_first[:, t, :], h[t][:, :PIECE], lam_first[:], MULT)
 
         pieces = S // PIECE
         lam_turned = psum.tile([P, P], F32, name="lam_turned", tag="b3")
@@ -167,21 +169,21 @@ def tile_picked_mixup_gelu_e_kernel(
         lam_col = keep.tile([P, pieces], F32, name="lam_col")
         nc.scalar.copy(out=lam_col[:], in_=lam_turned[:, :pieces])
 
-        own = []
-        scaled = []
+        own = {0: own_first}
+        scaled = {}
 
         def turn_back(n):
-            own.append(psum.tile([P, PACK, PIECE], F32, name=f"own{n}", tag=f"a{n}"))
+            own[n] = psum.tile([P, PACK, PIECE], F32, name=f"own{n}", tag=f"a{n}")
             for t in range(PACK):
                 nc.tensor.transpose(own[n][:, t, :], scaled[n][:, t, :], ident[:])
 
-        for n in range(pieces):
+        for n in range(1, pieces):
             turned = psum.tile([P, PACK, P], F32, name=f"turned{n}", tag=f"b{n}")
             for t in range(PACK):
                 nc.tensor.transpose(turned[:, t, :], h[t][:, n * PIECE : (n + 1) * PIECE], ident[:])
-            scaled.append(keep.tile([P, PACK, P], F32, name=f"scaled{n}"))
+            scaled[n] = keep.tile([P, PACK, P], F32, name=f"scaled{n}")
             nc.scalar.activation(out=scaled[n][:], in_=turned[:], func=COPY, scale=lam_col[:, n : n + 1])
-            if n > 0:
+            if n > 1:
                 turn_back(n - 1)
         turn_back(pieces - 1)
 
@@ -203,7 +205,7 @@ def tile_picked_mixup_gelu_e_kernel(
             nc.vector.quantize_mx(
                 out=z_codes[:].bitcast(FP8X4), scales=z_scales[:], in_=z_bf[n][:].rearrange("p c t -> p (c t)")
             )
-            y = psum.tile([P, N // P, PIECE], F32, name=f"y{n}", tag=f"b{n}")
+            y = psum.tile([P, N // P, PIECE], F32, name=f"y{n}", tag=f"b{pieces - 1 - n}")
             for b in range(N // P):
                 rows = slice(b * P, (b + 1) * P)
                 nc.tensor.matmul_mx(

@@ -24,8 +24,6 @@ K_PASS = P * PACK
 PASSES = K // K_PASS
 X_CHUNKS = ((0, 0, 512), (0, 512, 1024), (1, 0, 512), (1, 512, 768), (1, 768, 1024))
 X_SCALAR_SHARE = (256, 160, 256, 192, 96)
-W_CHUNKS = ((0, 0, 256), (0, 256, 512), (1, 0, 256), (1, 256, 384), (1, 384, 512))
-W_SCALAR_SHARE = (256, 256, 256, 0, 48)
 PIECE = 128
 H_COLS = S + 16
 
@@ -56,9 +54,11 @@ def tile_picked_mixup_gelu_e_kernel(
         ident = keep.tile([P, P], F32, name="ident")
         make_identity(nc, ident[:])
 
-        warm = keep.tile([P, 8], F32, name="warm")
-        nc.vector.memset(warm[:], 0.0)
-        nc.scalar.activation(out=warm[:], in_=warm[:], func=GELU)
+        h = [keep.tile([P, H_COLS], F32, name=f"h{t}") for t in range(PACK)]
+        zero = keep.tile([P, H_COLS - S], F32, name="zero")
+        nc.vector.memset(zero[:], 0.0)
+        for t in range(PACK):
+            nc.scalar.activation(out=h[t][:, S:], in_=zero[:], func=GELU)
 
         x_raw = []
         for n, (g, a, b) in enumerate(X_CHUNKS):
@@ -68,17 +68,17 @@ def tile_picked_mixup_gelu_e_kernel(
             if n == 0:
                 nc.sync.dma_start(offs_sb[:], offs)
         w_raw = []
-        for n, (g, a, b) in enumerate(W_CHUNKS):
-            w_raw.append(keep.tile([P, PACK, b - a], F32, name=f"w_raw{n}"))
-            rows = w1[g * K_PASS : (g + 1) * K_PASS, a:b]
-            nc.sync.dma_start(out=w_raw[n][:], in_=rows.rearrange("(p j) c -> p j c", j=PACK))
+        for g in range(PASSES):
+            w_raw.append(keep.tile([P, PACK, H], F32, name=f"w_raw{g}"))
+            rows = w1[g * K_PASS : (g + 1) * K_PASS, :]
+            nc.sync.dma_start(out=w_raw[g][:], in_=rows.rearrange("(p j) c -> p j c", j=PACK))
         nc.sync.dma_start(pos_sb[:], pos1)
         mu_sb = keep.tile([P, S], F32, name="mu_sb")
-        lam_rows = keep.tile([P, P], F32, name="lam_rows")
         nc.sync.dma_start(out=mu_sb[:], in_=mu)
-        nc.sync.dma_start(out=lam_rows[:], in_=lam.rearrange("a (n j) -> (a n) j", j=P)[:P, :])
-        lam_first = keep.tile([P, PIECE], F32, name="lam_first")
-        nc.sync.dma_start(out=lam_first[:], in_=lam[:, :PIECE])
+        pieces = S // PIECE
+        lam_col = keep.tile([P, pieces], F32, name="lam_col")
+        with nc.allow_non_contiguous_dma(reason="one share to a partition"):
+            nc.sync.dma_start(out=lam_col[:], in_=lam[0, :].rearrange("(n p) -> p n", p=PIECE))
         w2_codes = keep.tile([P, N], U32, name="w2_codes", align_bytes=64)
         nc.sync.dma_start(
             out=w2_codes[:].bitcast(I32), in_=w2_words[0].rearrange("p n t -> p (n t)").bitcast(I32)
@@ -111,23 +111,26 @@ def tile_picked_mixup_gelu_e_kernel(
 
         w_codes = [keep.tile([P, H], U32, name=f"w_codes{g}", align_bytes=64) for g in range(PASSES)]
         w_scales = keep.tile([P, H], U8, name="w_scales", align_bytes=64)
-        w_scales_early = keep.tile([P, P], U8, name="w_scales_early", align_bytes=64)
+        w_scales_early = keep.tile([P, 2 * P], U8, name="w_scales_early", align_bytes=64)
 
         def w_plane(g, cols):
-            if g == 0 and cols.stop <= P:
+            if g == 0 and cols.stop <= 2 * P:
                 return w_scales_early[:, cols]
             return w_scales[4 * g :, cols]
 
         w_bf = [keep.tile([P, PACK, P, PACK], BF16, name=f"w_bf{g}", align_bytes=64) for g in range(PASSES)]
-        for n, (g, a, b) in enumerate(W_CHUNKS):
-            split = W_SCALAR_SHARE[n]
-            for move, c0, c1 in ((on_scalar, 0, split), (on_vector, split, b - a)):
-                if c1 > c0:
-                    move(
-                        w_bf[g][:, :, (a + c0) // PACK : (a + c1) // PACK, :].rearrange("p t m j -> p m j t"),
-                        w_raw[n][:, :, c0:c1].rearrange("p j (m t) -> p m j t", t=PACK),
-                    )
-        for g, t0, t1 in ((0, 0, 1), (1, 0, 1), (1, 1, 2), (0, 1, 2), (1, 2, 4), (0, 2, 4)):
+        for move, g, t0, t1, m0, m1 in (
+            (on_scalar, 0, 0, 2, 0, P),
+            (on_scalar, 0, 2, 4, 0, P),
+            (on_vector, 1, 0, 2, 0, 96),
+            (on_scalar, 1, 0, 2, 96, P),
+            (on_scalar, 1, 2, 4, 0, P),
+        ):
+            move(
+                w_bf[g][:, t0:t1, m0:m1, :].rearrange("p t m j -> p m j t"),
+                w_raw[g][:].rearrange("p j (m t) -> p m j t", t=PACK)[:, m0:m1, :, t0:t1],
+            )
+        for g, t0, t1 in ((0, 0, 2), (1, 0, 1), (1, 1, 2), (1, 2, 4), (0, 2, 4)):
             cols = slice(t0 * P, t1 * P)
             nc.vector.quantize_mx(
                 out=w_codes[g][:, cols].bitcast(FP8X4),
@@ -135,11 +138,8 @@ def tile_picked_mixup_gelu_e_kernel(
                 in_=w_bf[g][:, t0:t1, :, :].rearrange("p t m j -> p (t m j)"),
             )
 
-        h = []
         for t in range(PACK):
             cols = slice(t * P, (t + 1) * P)
-            h_t = keep.tile([P, H_COLS], F32, name=f"h{t}")
-            nc.gpsimd.memset(h_t[:, S:], 0.0)
             parts = (("a0", 0, S // 2), ("b0", S // 2, S)) if t == 0 else ((f"a{t}", 0, S),)
             for tag, a, b in parts:
                 u = psum.tile([P, b - a], F32, name=f"u{t}{tag}", tag=tag)
@@ -153,23 +153,14 @@ def tile_picked_mixup_gelu_e_kernel(
                         start=(g == 0),
                         stop=(g == PASSES - 1),
                     )
-                nc.scalar.activation(out=h_t[:, a:b], in_=u[:], func=GELU)
-            h.append(h_t)
+                nc.scalar.activation(out=h[t][:, a:b], in_=u[:], func=GELU)
 
         out_view = out.rearrange("(b p) j -> p b j", p=P)
         partner = keep.tile([P, PACK, S], F32, name="partner")
-        own_first = keep.tile([P, PACK, PIECE], F32, name="own_first")
         for t in range(PACK):
             nc.vector.tensor_tensor(partner[:, t, :], h[t][:].indirect(pos_sb[:]), mu_sb[:], MULT)
-            nc.vector.tensor_tensor(own_first[:, t, :], h[t][:, :PIECE], lam_first[:], MULT)
 
-        pieces = S // PIECE
-        lam_turned = psum.tile([P, P], F32, name="lam_turned", tag="b3")
-        nc.tensor.transpose(lam_turned[:], lam_rows[:], ident[:])
-        lam_col = keep.tile([P, pieces], F32, name="lam_col")
-        nc.scalar.copy(out=lam_col[:], in_=lam_turned[:, :pieces])
-
-        own = {0: own_first}
+        own = {}
         scaled = {}
 
         def turn_back(n):
@@ -177,13 +168,13 @@ def tile_picked_mixup_gelu_e_kernel(
             for t in range(PACK):
                 nc.tensor.transpose(own[n][:, t, :], scaled[n][:, t, :], ident[:])
 
-        for n in range(1, pieces):
+        for n in range(pieces):
             turned = psum.tile([P, PACK, P], F32, name=f"turned{n}", tag=f"b{n}")
             for t in range(PACK):
                 nc.tensor.transpose(turned[:, t, :], h[t][:, n * PIECE : (n + 1) * PIECE], ident[:])
             scaled[n] = keep.tile([P, PACK, P], F32, name=f"scaled{n}")
             nc.scalar.activation(out=scaled[n][:], in_=turned[:], func=COPY, scale=lam_col[:, n : n + 1])
-            if n > 1:
+            if n > 0:
                 turn_back(n - 1)
         turn_back(pieces - 1)
 
@@ -205,11 +196,14 @@ def tile_picked_mixup_gelu_e_kernel(
             nc.vector.quantize_mx(
                 out=z_codes[:].bitcast(FP8X4), scales=z_scales[:], in_=z_bf[n][:].rearrange("p c t -> p (c t)")
             )
-            y = psum.tile([P, N // P, PIECE], F32, name=f"y{n}", tag=f"b{pieces - 1 - n}")
+            last = n == pieces - 1
+            y = [psum.tile([P, N // P, PIECE], F32, name=f"y{n}", tag=f"b{pieces - 1 - n}")] * 2
+            if last:
+                y[1] = psum.tile([P, N // P, PIECE], F32, name="y_last", tag="a0")
             for b in range(N // P):
                 rows = slice(b * P, (b + 1) * P)
                 nc.tensor.matmul_mx(
-                    out=y[:, b, :],
+                    out=y[b][:, b, :],
                     lhsT=w2_codes[:, rows].bitcast(FP8X4),
                     lhsT_scale=w2_scale_sb[:, rows],
                     rhs=z_codes[:].bitcast(FP8X4),
@@ -217,9 +211,15 @@ def tile_picked_mixup_gelu_e_kernel(
                     start=True,
                     stop=True,
                 )
-            y_sb = keep.tile([P, N // P, PIECE], F32, name=f"y_sb{n}")
-            nc.scalar.copy(out=y_sb[:], in_=y[:])
-            nc.sync.dma_start(out=out_view[:, :, cols], in_=y_sb[:])
+            if last:
+                for b, copy, queue in ((0, nc.scalar.copy, nc.scalar), (1, nc.vector.tensor_copy, nc.sync)):
+                    y_sb = keep.tile([P, PIECE], F32, name=f"y_last{b}")
+                    copy(out=y_sb[:], in_=y[b][:, b, :])
+                    queue.dma_start(out=out_view[:, b, cols], in_=y_sb[:])
+            else:
+                y_sb = keep.tile([P, N // P, PIECE], F32, name=f"y_sb{n}")
+                nc.scalar.copy(out=y_sb[:], in_=y[0][:])
+                nc.sync.dma_start(out=out_view[:, :, cols], in_=y_sb[:])
 
         for n in range(pieces + 1):
             if n < pieces:

@@ -22,8 +22,8 @@ P = 128
 PACK = 4
 K_PASS = P * PACK
 PASSES = K // K_PASS
-X_CHUNKS = ((0, 0, 512), (0, 512, 1024), (1, 0, 512), (1, 512, 768), (1, 768, 1024))
-X_SCALAR_SHARE = (256, 160, 256, 192, 96)
+X_LOADS = ((0, 0, 512), (0, 512, 1024), (1, 0, 512), (1, 512, 768), (1, 768, 1024))
+X_CHUNKS = ((0, 0, 512, 256), (1, 512, 768, 0), (1, 768, 1024, 176), (2, 0, 512, 288), (3, 512, 768, 192), (4, 768, 1024, 112))
 PIECE = 128
 H_COLS = S + 16
 
@@ -61,25 +61,25 @@ def tile_picked_mixup_gelu_e_kernel(
             nc.scalar.activation(out=h[t][:, S:], in_=zero[:], func=GELU)
 
         x_raw = []
-        for n, (g, a, b) in enumerate(X_CHUNKS):
-            x_raw.append(keep.tile([P, PACK, b - a], F32, name=f"x_raw{n}"))
+        for n, (g, a, b) in enumerate(X_LOADS):
+            x_raw.append(keep.tile([P, PACK, b - a], F32, name=f"x_raw{n}", align_bytes=256))
             rows = xT[g * K_PASS : (g + 1) * K_PASS, a:b]
             nc.sync.dma_start(out=x_raw[n][:], in_=rows.rearrange("(p j) c -> p j c", j=PACK))
             if n == 0:
                 nc.sync.dma_start(offs_sb[:], offs)
         w_raw = []
         for g in range(PASSES):
-            w_raw.append(keep.tile([P, PACK, H], F32, name=f"w_raw{g}"))
+            w_raw.append(keep.tile([P, PACK, H], F32, name=f"w_raw{g}", align_bytes=256))
             rows = w1[g * K_PASS : (g + 1) * K_PASS, :]
             nc.sync.dma_start(out=w_raw[g][:], in_=rows.rearrange("(p j) c -> p j c", j=PACK))
         nc.sync.dma_start(pos_sb[:], pos1)
-        mu_sb = keep.tile([P, S], F32, name="mu_sb")
+        mu_sb = keep.tile([P, S], F32, name="mu_sb", align_bytes=256)
         nc.sync.dma_start(out=mu_sb[:], in_=mu)
         pieces = S // PIECE
         lam_col = keep.tile([P, pieces], F32, name="lam_col")
         with nc.allow_non_contiguous_dma(reason="one share to a partition"):
             nc.sync.dma_start(out=lam_col[:], in_=lam[0, :].rearrange("(n p) -> p n", p=PIECE))
-        w2_codes = keep.tile([P, N], U32, name="w2_codes", align_bytes=64)
+        w2_codes = keep.tile([P, N], U32, name="w2_codes", align_bytes=256)
         nc.sync.dma_start(
             out=w2_codes[:].bitcast(I32), in_=w2_words[0].rearrange("p n t -> p (n t)").bitcast(I32)
         )
@@ -92,14 +92,15 @@ def tile_picked_mixup_gelu_e_kernel(
         x_words = [keep.tile([P, T], U32, name=f"x_words{g}", align_bytes=64) for g in range(PASSES)]
         picked_words = [keep.tile([P, S], U32, name=f"picked_words{g}", align_bytes=64) for g in range(PASSES)]
         picked_scales = keep.tile([P, S], U8, name="picked_scales", align_bytes=64)
-        for n, (g, c0, c1) in enumerate(X_CHUNKS):
+        for n, (load, c0, c1, split) in enumerate(X_CHUNKS):
+            g, first, last = X_LOADS[load]
             x_bf = keep.tile([P, c1 - c0, PACK], BF16, name=f"x_bf{n}", align_bytes=64)
-            split = X_SCALAR_SHARE[n]
             for move, a, b in ((on_scalar, 0, split), (on_vector, split, c1 - c0)):
-                move(
-                    x_bf[:, a:b, :].rearrange("p (c i) j -> p c j i", i=4),
-                    x_raw[n][:, :, a:b].rearrange("p j (c i) -> p c j i", i=4),
-                )
+                if b > a:
+                    move(
+                        x_bf[:, a:b, :].rearrange("p (c i) j -> p c j i", i=4),
+                        x_raw[load][:, :, c0 - first + a : c0 - first + b].rearrange("p j (c i) -> p c j i", i=4),
+                    )
             nc.vector.quantize_mx(
                 out=x_words[g][:, c0:c1].bitcast(FP8X4),
                 scales=x_scales[4 * g :, c0:c1],
@@ -130,7 +131,7 @@ def tile_picked_mixup_gelu_e_kernel(
                 w_bf[g][:, t0:t1, m0:m1, :].rearrange("p t m j -> p m j t"),
                 w_raw[g][:].rearrange("p j (m t) -> p m j t", t=PACK)[:, m0:m1, :, t0:t1],
             )
-        for g, t0, t1 in ((0, 0, 2), (1, 0, 1), (1, 1, 2), (1, 2, 4), (0, 2, 4)):
+        for g, t0, t1 in ((0, 0, 1), (0, 1, 2), (1, 0, 1), (1, 1, 2), (1, 2, 4), (0, 2, 4)):
             cols = slice(t0 * P, t1 * P)
             nc.vector.quantize_mx(
                 out=w_codes[g][:, cols].bitcast(FP8X4),
@@ -213,11 +214,11 @@ def tile_picked_mixup_gelu_e_kernel(
                 )
             if last:
                 for b, copy, queue in ((0, nc.scalar.copy, nc.scalar), (1, nc.vector.tensor_copy, nc.sync)):
-                    y_sb = keep.tile([P, PIECE], F32, name=f"y_last{b}")
+                    y_sb = keep.tile([P, PIECE], F32, name=f"y_last{b}", align_bytes=256)
                     copy(out=y_sb[:], in_=y[b][:, b, :])
                     queue.dma_start(out=out_view[:, b, cols], in_=y_sb[:])
             else:
-                y_sb = keep.tile([P, N // P, PIECE], F32, name=f"y_sb{n}")
+                y_sb = keep.tile([P, N // P, PIECE], F32, name=f"y_sb{n}", align_bytes=256)
                 nc.scalar.copy(out=y_sb[:], in_=y[0][:])
                 nc.sync.dma_start(out=out_view[:, :, cols], in_=y_sb[:])
 

@@ -22,9 +22,25 @@ P = 128
 PACK = 4
 K_PASS = P * PACK
 PASSES = K // K_PASS
-X_LOADS = ((0, 0, 512), (0, 512, 1024), (1, 0, 512), (1, 512, 768), (1, 768, 1024))
-X_CHUNKS = ((0, 0, 512, 256), (1, 512, 768, 0), (1, 768, 1024, 176), (2, 0, 512, 288), (3, 512, 768, 192), (4, 768, 1024, 112))
+SCALE_ROWS = 4
+LINE = 4
+MX_ALIGN = 64
+DMA_ALIGN = 256
+
+QUARTER = T // 4
+X_LOADS = (
+    (0, 0, 2 * QUARTER, QUARTER),
+    (0, 2 * QUARTER, 3 * QUARTER, QUARTER // 2),
+    (0, 3 * QUARTER, T, 3 * QUARTER // 8),
+    (1, 0, QUARTER, QUARTER),
+    (1, QUARTER, 2 * QUARTER, QUARTER),
+    (1, 2 * QUARTER, 3 * QUARTER, QUARTER // 2),
+    (1, 3 * QUARTER, T, 3 * QUARTER // 8),
+)
+W_LOADS = ((0, 0, H), (1, 0, H - P), (1, H - P, H))
+EARLY_TILES = 2
 PIECE = 128
+PIECES = S // PIECE
 H_COLS = S + 16
 
 
@@ -46,8 +62,8 @@ def tile_picked_mixup_gelu_e_kernel(
         offs_sb = keep.tile([P, S // 16], U16, name="offs_sb")
         pos_sb = keep.tile([P, S // 16], U16, name="pos_sb")
 
-        x_scales = keep.tile([P, T], U8, name="x_scales", align_bytes=64)
-        w2_scale_sb = keep.tile([P, N], U8, name="w2_scale_sb", align_bytes=64)
+        x_scales = keep.tile([P, T], U8, name="x_scales", align_bytes=MX_ALIGN)
+        w2_scale_sb = keep.tile([P, N], U8, name="w2_scale_sb", align_bytes=MX_ALIGN)
         nc.gpsimd.memset(x_scales[:], 0)
         nc.gpsimd.memset(w2_scale_sb[:], 0)
 
@@ -61,102 +77,102 @@ def tile_picked_mixup_gelu_e_kernel(
             nc.scalar.activation(out=h[t][:, S:], in_=zero[:], func=GELU)
 
         x_raw = []
-        for n, (g, a, b) in enumerate(X_LOADS):
-            x_raw.append(keep.tile([P, PACK, b - a], F32, name=f"x_raw{n}", align_bytes=256))
+        for n, (g, a, b, share) in enumerate(X_LOADS):
+            x_raw.append(keep.tile([P, PACK, b - a], F32, name=f"x_raw{n}", align_bytes=DMA_ALIGN))
             rows = xT[g * K_PASS : (g + 1) * K_PASS, a:b]
             nc.sync.dma_start(out=x_raw[n][:], in_=rows.rearrange("(p j) c -> p j c", j=PACK))
             if n == 0:
                 nc.sync.dma_start(offs_sb[:], offs)
         w_raw = []
-        for g in range(PASSES):
-            w_raw.append(keep.tile([P, PACK, H], F32, name=f"w_raw{g}", align_bytes=256))
-            rows = w1[g * K_PASS : (g + 1) * K_PASS, :]
-            nc.sync.dma_start(out=w_raw[g][:], in_=rows.rearrange("(p j) c -> p j c", j=PACK))
+        for n, (g, a, b) in enumerate(W_LOADS):
+            w_raw.append(keep.tile([P, PACK, b - a], F32, name=f"w_raw{n}", align_bytes=DMA_ALIGN))
+            rows = w1[g * K_PASS : (g + 1) * K_PASS, a:b]
+            nc.sync.dma_start(out=w_raw[n][:], in_=rows.rearrange("(p j) c -> p j c", j=PACK))
         nc.sync.dma_start(pos_sb[:], pos1)
-        mu_sb = keep.tile([P, S], F32, name="mu_sb", align_bytes=256)
+        mu_sb = keep.tile([P, S], F32, name="mu_sb", align_bytes=DMA_ALIGN)
         nc.sync.dma_start(out=mu_sb[:], in_=mu)
-        pieces = S // PIECE
-        lam_col = keep.tile([P, pieces], F32, name="lam_col")
+        lam_col = keep.tile([P, PIECES], F32, name="lam_col")
         with nc.allow_non_contiguous_dma(reason="one share to a partition"):
             nc.sync.dma_start(out=lam_col[:], in_=lam[0, :].rearrange("(n p) -> p n", p=PIECE))
-        w2_codes = keep.tile([P, N], U32, name="w2_codes", align_bytes=256)
+        w2_codes = keep.tile([P, N], U32, name="w2_codes", align_bytes=DMA_ALIGN)
         nc.sync.dma_start(
             out=w2_codes[:].bitcast(I32), in_=w2_words[0].rearrange("p n t -> p (n t)").bitcast(I32)
         )
-        for q in range(4):
+        for q in range(P // 32):
             nc.sync.dma_start(
-                out=w2_scale_sb[32 * q : 32 * q + 4, :].bitcast(I32),
-                in_=w2_scales[0, 4 * q : 4 * q + 4, :].bitcast(I32),
+                out=w2_scale_sb[32 * q : 32 * q + SCALE_ROWS, :].bitcast(I32),
+                in_=w2_scales[0, SCALE_ROWS * q : SCALE_ROWS * (q + 1), :].bitcast(I32),
             )
 
-        x_words = [keep.tile([P, T], U32, name=f"x_words{g}", align_bytes=64) for g in range(PASSES)]
-        picked_words = [keep.tile([P, S], U32, name=f"picked_words{g}", align_bytes=64) for g in range(PASSES)]
-        picked_scales = keep.tile([P, S], U8, name="picked_scales", align_bytes=64)
-        for n, (load, c0, c1, split) in enumerate(X_CHUNKS):
-            g, first, last = X_LOADS[load]
-            x_bf = keep.tile([P, c1 - c0, PACK], BF16, name=f"x_bf{n}", align_bytes=64)
-            for move, a, b in ((on_scalar, 0, split), (on_vector, split, c1 - c0)):
-                if b > a:
+        x_words = [keep.tile([P, T], U32, name=f"x_words{g}", align_bytes=MX_ALIGN) for g in range(PASSES)]
+        picked_words = [keep.tile([P, S], U32, name=f"picked_words{g}", align_bytes=MX_ALIGN) for g in range(PASSES)]
+        picked_scales = keep.tile([P, S], U8, name="picked_scales", align_bytes=MX_ALIGN)
+        for n, (g, a, b, share) in enumerate(X_LOADS):
+            x_bf = keep.tile([P, b - a, PACK], BF16, name=f"x_bf{n}", align_bytes=MX_ALIGN)
+            for move, c0, c1 in ((on_scalar, 0, share), (on_vector, share, b - a)):
+                if c1 > c0:
                     move(
-                        x_bf[:, a:b, :].rearrange("p (c i) j -> p c j i", i=4),
-                        x_raw[load][:, :, c0 - first + a : c0 - first + b].rearrange("p j (c i) -> p c j i", i=4),
+                        x_bf[:, c0:c1, :].rearrange("p (c i) j -> p c j i", i=LINE),
+                        x_raw[n][:, :, c0:c1].rearrange("p j (c i) -> p c j i", i=LINE),
                     )
             nc.vector.quantize_mx(
-                out=x_words[g][:, c0:c1].bitcast(FP8X4),
-                scales=x_scales[4 * g :, c0:c1],
+                out=x_words[g][:, a:b].bitcast(FP8X4),
+                scales=x_scales[SCALE_ROWS * g :, a:b],
                 in_=x_bf[:].rearrange("p c j -> p (c j)"),
             )
-            if c1 == T:
+            if b == T:
                 nc.vector.tensor_copy(out=picked_words[g][:], in_=x_words[g][:].indirect(offs_sb[:]))
         nc.vector.tensor_copy(out=picked_scales[:], in_=x_scales[:].indirect(offs_sb[:]))
 
-        w_codes = [keep.tile([P, H], U32, name=f"w_codes{g}", align_bytes=64) for g in range(PASSES)]
-        w_scales = keep.tile([P, H], U8, name="w_scales", align_bytes=64)
-        w_scales_early = keep.tile([P, 2 * P], U8, name="w_scales_early", align_bytes=64)
+        w_codes = [keep.tile([P, H], U32, name=f"w_codes{g}", align_bytes=MX_ALIGN) for g in range(PASSES)]
+        w_scales = keep.tile([P, H], U8, name="w_scales", align_bytes=MX_ALIGN)
+        w_scales_early = keep.tile([P, EARLY_TILES * P], U8, name="w_scales_early", align_bytes=MX_ALIGN)
 
-        def w_plane(g, cols):
-            if g == 0 and cols.stop <= 2 * P:
+        def w_scale_rows(g, cols):
+            if g == 0 and cols.stop <= EARLY_TILES * P:
                 return w_scales_early[:, cols]
-            return w_scales[4 * g :, cols]
+            return w_scales[SCALE_ROWS * g :, cols]
 
-        w_bf = [keep.tile([P, PACK, P, PACK], BF16, name=f"w_bf{g}", align_bytes=64) for g in range(PASSES)]
-        for move, g, t0, t1, m0, m1 in (
-            (on_scalar, 0, 0, 2, 0, P),
-            (on_scalar, 0, 2, 4, 0, P),
-            (on_vector, 1, 0, 2, 0, 96),
-            (on_scalar, 1, 0, 2, 96, P),
-            (on_scalar, 1, 2, 4, 0, P),
-        ):
-            move(
-                w_bf[g][:, t0:t1, m0:m1, :].rearrange("p t m j -> p m j t"),
-                w_raw[g][:].rearrange("p j (m t) -> p m j t", t=PACK)[:, m0:m1, :, t0:t1],
-            )
-        for g, t0, t1 in ((0, 0, 1), (0, 1, 2), (1, 0, 1), (1, 1, 2), (1, 2, 4), (0, 2, 4)):
+        w_bf = [keep.tile([P, PACK, P, PACK], BF16, name=f"w_bf{g}", align_bytes=MX_ALIGN) for g in range(PASSES)]
+        for tiles in (slice(0, EARLY_TILES), slice(EARLY_TILES, PACK)):
+            for n, (g, a, b) in enumerate(W_LOADS):
+                move = on_vector if g == 1 and tiles.start == 0 else on_scalar
+                move(
+                    w_bf[g][:, tiles, a // PACK : b // PACK, :].rearrange("p t m j -> p m j t"),
+                    w_raw[n][:].rearrange("p j (m t) -> p m j t", t=PACK)[:, :, :, tiles],
+                )
+
+        def quantise_weights(g, t0, t1):
             cols = slice(t0 * P, t1 * P)
             nc.vector.quantize_mx(
                 out=w_codes[g][:, cols].bitcast(FP8X4),
-                scales=w_plane(g, cols),
+                scales=w_scale_rows(g, cols),
                 in_=w_bf[g][:, t0:t1, :, :].rearrange("p t m j -> p (t m j)"),
             )
+
+        for g in range(PASSES):
+            for t in range(EARLY_TILES):
+                quantise_weights(g, t, t + 1)
+        for g in reversed(range(PASSES)):
+            quantise_weights(g, EARLY_TILES, PACK)
 
         for t in range(PACK):
             cols = slice(t * P, (t + 1) * P)
             parts = (("a0", 0, S // 2), ("b0", S // 2, S)) if t == 0 else ((f"a{t}", 0, S),)
-            for tag, a, b in parts:
-                u = psum.tile([P, b - a], F32, name=f"u{t}{tag}", tag=tag)
+            for bank, a, b in parts:
+                u = psum.tile([P, b - a], F32, name=f"u{t}{bank}", tag=bank)
                 for g in range(PASSES):
                     nc.tensor.matmul_mx(
                         out=u[:],
                         lhsT=w_codes[g][:, cols].bitcast(FP8X4),
-                        lhsT_scale=w_plane(g, cols),
+                        lhsT_scale=w_scale_rows(g, cols),
                         rhs=picked_words[g][:, a:b].bitcast(FP8X4),
-                        rhs_scale=picked_scales[4 * g :, a:b],
+                        rhs_scale=picked_scales[SCALE_ROWS * g :, a:b],
                         start=(g == 0),
                         stop=(g == PASSES - 1),
                     )
                 nc.scalar.activation(out=h[t][:, a:b], in_=u[:], func=GELU)
 
-        out_view = out.rearrange("(b p) j -> p b j", p=P)
         partner = keep.tile([P, PACK, S], F32, name="partner")
         for t in range(PACK):
             nc.vector.tensor_tensor(partner[:, t, :], h[t][:].indirect(pos_sb[:]), mu_sb[:], MULT)
@@ -169,7 +185,7 @@ def tile_picked_mixup_gelu_e_kernel(
             for t in range(PACK):
                 nc.tensor.transpose(own[n][:, t, :], scaled[n][:, t, :], ident[:])
 
-        for n in range(pieces):
+        for n in range(PIECES):
             turned = psum.tile([P, PACK, P], F32, name=f"turned{n}", tag=f"b{n}")
             for t in range(PACK):
                 nc.tensor.transpose(turned[:, t, :], h[t][:, n * PIECE : (n + 1) * PIECE], ident[:])
@@ -177,34 +193,35 @@ def tile_picked_mixup_gelu_e_kernel(
             nc.scalar.activation(out=scaled[n][:], in_=turned[:], func=COPY, scale=lam_col[:, n : n + 1])
             if n > 0:
                 turn_back(n - 1)
-        turn_back(pieces - 1)
+        turn_back(PIECES - 1)
 
-        z_bf = [keep.tile([P, PIECE, PACK], BF16, name=f"z_bf{n}", align_bytes=64) for n in range(pieces)]
+        out_view = out.rearrange("(r p) j -> p r j", p=P)
+        z_bf = [keep.tile([P, PIECE, PACK], BF16, name=f"z_bf{n}", align_bytes=MX_ALIGN) for n in range(PIECES)]
 
         def mix(n):
             cols = slice(n * PIECE, (n + 1) * PIECE)
             nc.vector.tensor_tensor(
-                z_bf[n][:].rearrange("p (c i) t -> p c t i", i=4),
-                own[n][:].rearrange("p t (c i) -> p c t i", i=4),
-                partner[:, :, cols].rearrange("p t (c i) -> p c t i", i=4),
+                z_bf[n][:].rearrange("p (c i) t -> p c t i", i=LINE),
+                own[n][:].rearrange("p t (c i) -> p c t i", i=LINE),
+                partner[:, :, cols].rearrange("p t (c i) -> p c t i", i=LINE),
                 ADD,
             )
 
         def second_product(n):
             cols = slice(n * PIECE, (n + 1) * PIECE)
-            z_codes = keep.tile([P, PIECE], U32, name=f"z_codes{n}", align_bytes=64)
-            z_scales = keep.tile([P, PIECE], U8, name=f"z_scales{n}", align_bytes=64)
+            z_codes = keep.tile([P, PIECE], U32, name=f"z_codes{n}", align_bytes=MX_ALIGN)
+            z_scales = keep.tile([P, PIECE], U8, name=f"z_scales{n}", align_bytes=MX_ALIGN)
             nc.vector.quantize_mx(
                 out=z_codes[:].bitcast(FP8X4), scales=z_scales[:], in_=z_bf[n][:].rearrange("p c t -> p (c t)")
             )
-            last = n == pieces - 1
-            y = [psum.tile([P, N // P, PIECE], F32, name=f"y{n}", tag=f"b{pieces - 1 - n}")] * 2
+            last = n == PIECES - 1
+            y = [psum.tile([P, N // P, PIECE], F32, name=f"y{n}", tag=f"b{PIECES - 1 - n}")] * 2
             if last:
-                y[1] = psum.tile([P, N // P, PIECE], F32, name="y_last", tag="a0")
-            for b in range(N // P):
-                rows = slice(b * P, (b + 1) * P)
+                y[1] = psum.tile([P, N // P, PIECE], F32, name="y_second", tag="a0")
+            for r in range(N // P):
+                rows = slice(r * P, (r + 1) * P)
                 nc.tensor.matmul_mx(
-                    out=y[b][:, b, :],
+                    out=y[r][:, r, :],
                     lhsT=w2_codes[:, rows].bitcast(FP8X4),
                     lhsT_scale=w2_scale_sb[:, rows],
                     rhs=z_codes[:].bitcast(FP8X4),
@@ -213,17 +230,17 @@ def tile_picked_mixup_gelu_e_kernel(
                     stop=True,
                 )
             if last:
-                for b, copy, queue in ((0, nc.scalar.copy, nc.scalar), (1, nc.vector.tensor_copy, nc.sync)):
-                    y_sb = keep.tile([P, PIECE], F32, name=f"y_last{b}", align_bytes=256)
-                    copy(out=y_sb[:], in_=y[b][:, b, :])
-                    queue.dma_start(out=out_view[:, b, cols], in_=y_sb[:])
+                for r, copy, queue in ((0, nc.scalar.copy, nc.scalar), (1, nc.vector.tensor_copy, nc.sync)):
+                    y_sb = keep.tile([P, PIECE], F32, name=f"y_last{r}", align_bytes=DMA_ALIGN)
+                    copy(out=y_sb[:], in_=y[r][:, r, :])
+                    queue.dma_start(out=out_view[:, r, cols], in_=y_sb[:])
             else:
-                y_sb = keep.tile([P, N // P, PIECE], F32, name=f"y_sb{n}", align_bytes=256)
+                y_sb = keep.tile([P, N // P, PIECE], F32, name=f"y_sb{n}", align_bytes=DMA_ALIGN)
                 nc.scalar.copy(out=y_sb[:], in_=y[0][:])
                 nc.sync.dma_start(out=out_view[:, :, cols], in_=y_sb[:])
 
-        for n in range(pieces + 1):
-            if n < pieces:
+        for n in range(PIECES + 1):
+            if n < PIECES:
                 mix(n)
             if n > 0:
                 second_product(n - 1)

@@ -29,13 +29,12 @@ DMA_ALIGN = 256
 
 QUARTER = T // 4
 X_LOADS = (
-    (0, 0, 2 * QUARTER, QUARTER),
-    (0, 2 * QUARTER, 3 * QUARTER, QUARTER // 2),
-    (0, 3 * QUARTER, T, 3 * QUARTER // 8),
-    (1, 0, QUARTER, QUARTER),
-    (1, QUARTER, 2 * QUARTER, QUARTER),
-    (1, 2 * QUARTER, 3 * QUARTER, QUARTER // 2),
-    (1, 3 * QUARTER, T, 3 * QUARTER // 8),
+    (0, 0, 2 * QUARTER, 4),
+    (0, 2 * QUARTER, T, 3),
+    (1, 0, QUARTER, 8),
+    (1, QUARTER, 2 * QUARTER, 8),
+    (1, 2 * QUARTER, 3 * QUARTER, 4),
+    (1, 3 * QUARTER, T, 3),
 )
 W_LOADS = ((0, 0, H), (1, 0, H - P), (1, H - P, H))
 EARLY_TILES = 2
@@ -77,7 +76,7 @@ def tile_picked_mixup_gelu_e_kernel(
             nc.scalar.activation(out=h[t][:, S:], in_=zero[:], func=GELU)
 
         x_raw = []
-        for n, (g, a, b, share) in enumerate(X_LOADS):
+        for n, (g, a, b, eighths) in enumerate(X_LOADS):
             x_raw.append(keep.tile([P, PACK, b - a], F32, name=f"x_raw{n}", align_bytes=DMA_ALIGN))
             rows = xT[g * K_PASS : (g + 1) * K_PASS, a:b]
             nc.sync.dma_start(out=x_raw[n][:], in_=rows.rearrange("(p j) c -> p j c", j=PACK))
@@ -107,8 +106,9 @@ def tile_picked_mixup_gelu_e_kernel(
         x_words = [keep.tile([P, T], U32, name=f"x_words{g}", align_bytes=MX_ALIGN) for g in range(PASSES)]
         picked_words = [keep.tile([P, S], U32, name=f"picked_words{g}", align_bytes=MX_ALIGN) for g in range(PASSES)]
         picked_scales = keep.tile([P, S], U8, name="picked_scales", align_bytes=MX_ALIGN)
-        for n, (g, a, b, share) in enumerate(X_LOADS):
+        for n, (g, a, b, eighths) in enumerate(X_LOADS):
             x_bf = keep.tile([P, b - a, PACK], BF16, name=f"x_bf{n}", align_bytes=MX_ALIGN)
+            share = (b - a) * eighths // 8
             for move, c0, c1 in ((on_scalar, 0, share), (on_vector, share, b - a)):
                 if c1 > c0:
                     move(
@@ -230,10 +230,10 @@ def tile_picked_mixup_gelu_e_kernel(
                     stop=True,
                 )
             if last:
-                for r, copy, queue in ((0, nc.scalar.copy, nc.scalar), (1, nc.vector.tensor_copy, nc.sync)):
+                for r, copy in enumerate((nc.scalar.copy, nc.vector.tensor_copy)):
                     y_sb = keep.tile([P, PIECE], F32, name=f"y_last{r}", align_bytes=DMA_ALIGN)
                     copy(out=y_sb[:], in_=y[r][:, r, :])
-                    queue.dma_start(out=out_view[:, r, cols], in_=y_sb[:])
+                    nc.sync.dma_start(out=out_view[:, r, cols], in_=y_sb[:])
             else:
                 y_sb = keep.tile([P, N // P, PIECE], F32, name=f"y_sb{n}", align_bytes=DMA_ALIGN)
                 nc.scalar.copy(out=y_sb[:], in_=y[0][:])

@@ -34,7 +34,8 @@ X_LOADS = (
     (1, 0, QUARTER, 8),
     (1, QUARTER, 2 * QUARTER, 8),
     (1, 2 * QUARTER, 3 * QUARTER, 4),
-    (1, 3 * QUARTER, T, 3),
+    (1, 3 * QUARTER, T - QUARTER // 2, 8),
+    (1, T - QUARTER // 2, T, 0),
 )
 W_LOADS = ((0, 0, H), (1, 0, H - P), (1, H - P, H))
 EARLY_TILES = 2

@@ -85,7 +85,7 @@ def tile_picked_mixup_gelu_e_kernel(
                 nc.sync.dma_start(offs_sb[:], offs)
         w_raw = []
         for n, (g, a, b) in enumerate(W_LOADS):
-            w_raw.append(keep.tile([P, PACK, b - a], F32, name=f"w_raw{n}", align_bytes=DMA_ALIGN))
+            w_raw.append(keep.tile([P, PACK, b - a], F32, name=f"w_raw{n}", tag=f"w_raw{n}", align_bytes=DMA_ALIGN))
             rows = w1[g * K_PASS : (g + 1) * K_PASS, a:b]
             nc.sync.dma_start(out=w_raw[n][:], in_=rows.rearrange("(p j) c -> p j c", j=PACK))
         nc.sync.dma_start(pos_sb[:], pos1)
@@ -125,7 +125,7 @@ def tile_picked_mixup_gelu_e_kernel(
                 nc.vector.tensor_copy(out=picked_words[g][:], in_=x_words[g][:].indirect(offs_sb[:]))
         nc.vector.tensor_copy(out=picked_scales[:], in_=x_scales[:].indirect(offs_sb[:]))
 
-        w_codes = [keep.tile([P, H], U32, name=f"w_codes{g}", align_bytes=MX_ALIGN) for g in range(PASSES)]
+        w_codes = {}
         w_scales = keep.tile([P, H], U8, name="w_scales", align_bytes=MX_ALIGN)
         w_scales_early = keep.tile([P, EARLY_TILES * P], U8, name="w_scales_early", align_bytes=MX_ALIGN)
 
@@ -134,27 +134,52 @@ def tile_picked_mixup_gelu_e_kernel(
                 return w_scales_early[:, cols]
             return w_scales[SCALE_ROWS * g :, cols]
 
-        w_bf = [keep.tile([P, PACK, P, PACK], BF16, name=f"w_bf{g}", align_bytes=MX_ALIGN) for g in range(PASSES)]
-        for tiles in (slice(0, EARLY_TILES), slice(EARLY_TILES, PACK)):
-            for n, (g, a, b) in enumerate(W_LOADS):
-                move = on_vector if g == 1 and tiles.start == 0 else on_scalar
-                move(
-                    w_bf[g][:, tiles, a // PACK : b // PACK, :].rearrange("p t m j -> p m j t"),
-                    w_raw[n][:].rearrange("p j (m t) -> p m j t", t=PACK)[:, :, :, tiles],
-                )
+        w_bf = {
+            (g, t0): keep.tile(
+                [P, EARLY_TILES, P, PACK], BF16, name=f"w_bf{g}{t0}", tag=f"w_bf{g}{t0}", align_bytes=MX_ALIGN
+            )
+            for g in range(PASSES)
+            for t0 in (0, EARLY_TILES)
+        }
+
+        def on_gpsimd(dst, src):
+            nc.gpsimd.tensor_scalar(dst, src, 1.0, 0.0, MULT, ADD)
+
+        def round_weights(move, n, tiles, c0, c1):
+            g, a, b = W_LOADS[n]
+            dst = w_bf[g, tiles.start][:, :, c0 // PACK : c1 // PACK, :]
+            src = w_raw[n][:, :, c0 - a : c1 - a].rearrange("p j (m t) -> p t m j", t=PACK)[:, tiles, :, :]
+            if move != on_gpsimd:
+                dst, src = dst.rearrange("p t m j -> p m j t"), src.rearrange("p t m j -> p m j t")
+            move(dst, src)
+
+        early, late = slice(0, EARLY_TILES), slice(EARLY_TILES, PACK)
+        round_weights(on_scalar, 0, early, 0, H)
+        round_weights(on_gpsimd, 0, late, 0, H - P)
+        round_weights(on_scalar, 0, late, H - P, H)
+        round_weights(on_scalar, 1, early, 0, H // 2)
+        round_weights(on_vector, 1, early, H // 2, H - P)
+        round_weights(on_vector, 2, early, H - P, H)
+        round_weights(on_scalar, 1, late, 0, H - P)
+        round_weights(on_scalar, 2, late, H - P, H)
 
         def quantise_weights(g, t0, t1):
             cols = slice(t0 * P, t1 * P)
+            base = t0 // EARLY_TILES * EARLY_TILES
+            tag = "w_bf10" if g == 0 and t0 >= EARLY_TILES else f"w_codes{g}{t0}"
+            codes = keep.tile([P, (t1 - t0) * P], U32, name=f"w_codes{g}{t0}", tag=tag, align_bytes=MX_ALIGN)
+            for t in range(t0, t1):
+                w_codes[g, t] = codes[:, (t - t0) * P : (t - t0 + 1) * P]
             nc.vector.quantize_mx(
-                out=w_codes[g][:, cols].bitcast(FP8X4),
+                out=codes[:].bitcast(FP8X4),
                 scales=w_scale_rows(g, cols),
-                in_=w_bf[g][:, t0:t1, :, :].rearrange("p t m j -> p (t m j)"),
+                in_=w_bf[g, base][:, t0 - base : t1 - base, :, :].rearrange("p t m j -> p (t m j)"),
             )
 
         for g in range(PASSES):
             for t in range(EARLY_TILES):
                 quantise_weights(g, t, t + 1)
-        for g in reversed(range(PASSES)):
+        for g in range(PASSES):
             quantise_weights(g, EARLY_TILES, PACK)
 
         for t in range(PACK):
@@ -165,7 +190,7 @@ def tile_picked_mixup_gelu_e_kernel(
                 for g in range(PASSES):
                     nc.tensor.matmul_mx(
                         out=u[:],
-                        lhsT=w_codes[g][:, cols].bitcast(FP8X4),
+                        lhsT=w_codes[g, t].bitcast(FP8X4),
                         lhsT_scale=w_scale_rows(g, cols),
                         rhs=picked_words[g][:, a:b].bitcast(FP8X4),
                         rhs_scale=picked_scales[SCALE_ROWS * g :, a:b],

@@ -37,7 +37,7 @@ X_LOADS = (
     (1, 3 * QUARTER, T - QUARTER // 2, 8),
     (1, T - QUARTER // 2, T, 0),
 )
-W_LOADS = ((0, 0, H), (1, 0, H - P), (1, H - P, H))
+W_LOADS = ((0, 0, H // 2), (0, H // 2, H), (1, 0, H // 2), (1, H // 2, H - P), (1, H - P, H))
 EARLY_TILES = 2
 PIECE = 128
 PIECES = S // PIECE
@@ -145,23 +145,18 @@ def tile_picked_mixup_gelu_e_kernel(
         def on_gpsimd(dst, src):
             nc.gpsimd.tensor_scalar(dst, src, 1.0, 0.0, MULT, ADD)
 
-        def round_weights(move, n, tiles, c0, c1):
+        def round_weights(move, n, t0):
             g, a, b = W_LOADS[n]
-            dst = w_bf[g, tiles.start][:, :, c0 // PACK : c1 // PACK, :]
-            src = w_raw[n][:, :, c0 - a : c1 - a].rearrange("p j (m t) -> p t m j", t=PACK)[:, tiles, :, :]
+            dst = w_bf[g, t0][:, :, a // PACK : b // PACK, :]
+            src = w_raw[n][:].rearrange("p j (m t) -> p t m j", t=PACK)[:, t0 : t0 + EARLY_TILES, :, :]
             if move != on_gpsimd:
                 dst, src = dst.rearrange("p t m j -> p m j t"), src.rearrange("p t m j -> p m j t")
             move(dst, src)
 
-        early, late = slice(0, EARLY_TILES), slice(EARLY_TILES, PACK)
-        round_weights(on_scalar, 0, early, 0, H)
-        round_weights(on_gpsimd, 0, late, 0, H - P)
-        round_weights(on_scalar, 0, late, H - P, H)
-        round_weights(on_scalar, 1, early, 0, H // 2)
-        round_weights(on_vector, 1, early, H // 2, H - P)
-        round_weights(on_vector, 2, early, H - P, H)
-        round_weights(on_scalar, 1, late, 0, H - P)
-        round_weights(on_scalar, 2, late, H - P, H)
+        for n, (g, a, b) in enumerate(W_LOADS):
+            round_weights(on_vector if b - a == P else on_scalar, n, 0)
+        for n, (g, a, b) in enumerate(W_LOADS):
+            round_weights(on_gpsimd if g == 0 else on_scalar, n, EARLY_TILES)
 
         def quantise_weights(g, t0, t1):
             cols = slice(t0 * P, t1 * P)
@@ -224,6 +219,8 @@ def tile_picked_mixup_gelu_e_kernel(
         out_view = out.rearrange("(r p) j -> p r j", p=P)
         z_bf = [keep.tile([P, PIECE, PACK], BF16, name=f"z_bf{n}", align_bytes=MX_ALIGN) for n in range(PIECES)]
 
+        y_sb = keep.tile([P, N // P, S], F32, name="y_sb", align_bytes=DMA_ALIGN)
+
         def mix(n):
             cols = slice(n * PIECE, (n + 1) * PIECE)
             nc.vector.tensor_tensor(
@@ -257,13 +254,12 @@ def tile_picked_mixup_gelu_e_kernel(
                 )
             if last:
                 for r, copy in enumerate((nc.scalar.copy, nc.vector.tensor_copy)):
-                    y_sb = keep.tile([P, PIECE], F32, name=f"y_last{r}", align_bytes=DMA_ALIGN)
-                    copy(out=y_sb[:], in_=y[r][:, r, :])
-                    nc.sync.dma_start(out=out_view[:, r, cols], in_=y_sb[:])
+                    copy(out=y_sb[:, r, cols], in_=y[r][:, r, :])
             else:
-                y_sb = keep.tile([P, N // P, PIECE], F32, name=f"y_sb{n}", align_bytes=DMA_ALIGN)
-                nc.scalar.copy(out=y_sb[:], in_=y[0][:])
-                nc.sync.dma_start(out=out_view[:, :, cols], in_=y_sb[:])
+                nc.scalar.copy(out=y_sb[:, :, cols], in_=y[0][:])
+            if n > 0:
+                stored = slice(0 if n == 1 else cols.start, cols.stop)
+                nc.sync.dma_start(out=out_view[:, :, stored], in_=y_sb[:, :, stored])
 
         for n in range(PIECES + 1):
             if n < PIECES:

@@ -122,8 +122,21 @@ def tile_picked_mixup_gelu_e_kernel(
                 in_=x_bf[:].rearrange("p c j -> p (c j)"),
             )
             if b == T:
+                if g == PASSES - 1:
+                    nc.vector.tensor_copy(out=picked_scales[:], in_=x_scales[:].indirect(offs_sb[:]))
                 nc.vector.tensor_copy(out=picked_words[g][:], in_=x_words[g][:].indirect(offs_sb[:]))
-        nc.vector.tensor_copy(out=picked_scales[:], in_=x_scales[:].indirect(offs_sb[:]))
+
+        for bank in ("b2", "b3"):
+            warm = psum.tile([P, S], F32, name=f"warm_{bank}", tag=bank)
+            nc.tensor.matmul_mx(
+                out=warm[:],
+                lhsT=picked_words[0][:, :P].bitcast(FP8X4),
+                lhsT_scale=picked_scales[:, :P],
+                rhs=picked_words[0][:].bitcast(FP8X4),
+                rhs_scale=picked_scales[:],
+                start=True,
+                stop=True,
+            )
 
         w_codes = {}
         w_scales = keep.tile([P, H], U8, name="w_scales", align_bytes=MX_ALIGN)

@@ -126,14 +126,14 @@ def tile_picked_mixup_gelu_e_kernel(
                     nc.vector.tensor_copy(out=picked_scales[:], in_=x_scales[:].indirect(offs_sb[:]))
                 nc.vector.tensor_copy(out=picked_words[g][:], in_=x_words[g][:].indirect(offs_sb[:]))
 
-        for bank in ("b2", "b3"):
-            warm = psum.tile([P, S], F32, name=f"warm_{bank}", tag=bank)
+        for bank, width in (("b2", S), ("b3", S), ("b1", S // 2)):
+            warm = psum.tile([P, width], F32, name=f"warm_{bank}", tag=bank)
             nc.tensor.matmul_mx(
                 out=warm[:],
                 lhsT=picked_words[0][:, :P].bitcast(FP8X4),
                 lhsT_scale=picked_scales[:, :P],
-                rhs=picked_words[0][:].bitcast(FP8X4),
-                rhs_scale=picked_scales[:],
+                rhs=picked_words[0][:, :width].bitcast(FP8X4),
+                rhs_scale=picked_scales[:, :width],
                 start=True,
                 stop=True,
             )

@@ -24,24 +24,17 @@ K_PASS = P * PACK
 PASSES = K // K_PASS
 SCALE_ROWS = 4
 LINE = 4
+LIST_ROWS = 16
 MX_ALIGN = 64
 DMA_ALIGN = 256
 
-QUARTER = T // 4
-X_LOADS = (
-    (0, 0, 2 * QUARTER, 4),
-    (0, 2 * QUARTER, T, 3),
-    (1, 0, QUARTER, 8),
-    (1, QUARTER, 2 * QUARTER, 8),
-    (1, 2 * QUARTER, 3 * QUARTER, 4),
-    (1, 3 * QUARTER, T - QUARTER // 2, 8),
-    (1, T - QUARTER // 2, T, 0),
-)
+X_LOADS = ((0, 0, 2), (0, 2, 2), (1, 0, 2), (1, 2, 1), (1, 3, 1))
 W_LOADS = ((0, 0, H // 2), (0, H // 2, H), (1, 0, H // 2), (1, H // 2, H - P), (1, H - P, H))
-EARLY_TILES = 2
 PIECE = 128
 PIECES = S // PIECE
+HALF = S // 2
 H_COLS = S + 16
+SCALAR_TILE = 2
 
 
 def tile_picked_mixup_gelu_e_kernel(
@@ -59,12 +52,10 @@ def tile_picked_mixup_gelu_e_kernel(
         keep = ctx.enter_context(tc.tile_pool(name="keep", bufs=1))
         psum = ctx.enter_context(tc.psum_pool(name="psum", bufs=1))
 
-        offs_sb = keep.tile([P, S // 16], U16, name="offs_sb")
-        pos_sb = keep.tile([P, S // 16], U16, name="pos_sb")
+        offs_sb = keep.tile([P, S // LIST_ROWS], U16, name="offs_sb")
+        pos_sb = keep.tile([P, S // LIST_ROWS], U16, name="pos_sb")
 
-        x_scales = keep.tile([P, T], U8, name="x_scales", align_bytes=MX_ALIGN)
         w2_scale_sb = keep.tile([P, N], U8, name="w2_scale_sb", align_bytes=MX_ALIGN)
-        nc.gpsimd.memset(x_scales[:], 0)
         nc.gpsimd.memset(w2_scale_sb[:], 0)
 
         ident = keep.tile([P, P], F32, name="ident")
@@ -77,15 +68,15 @@ def tile_picked_mixup_gelu_e_kernel(
             nc.scalar.activation(out=h[t][:, S:], in_=zero[:], func=GELU)
 
         x_raw = []
-        for n, (g, a, b, eighths) in enumerate(X_LOADS):
-            x_raw.append(keep.tile([P, PACK, b - a], F32, name=f"x_raw{n}", align_bytes=DMA_ALIGN))
-            rows = xT[g * K_PASS : (g + 1) * K_PASS, a:b]
-            nc.sync.dma_start(out=x_raw[n][:], in_=rows.rearrange("(p j) c -> p j c", j=PACK))
+        for n, (g, j0, planes) in enumerate(X_LOADS):
+            x_raw.append(keep.tile([P, planes * T], F32, name=f"x_raw{n}", align_bytes=DMA_ALIGN))
+            rows = xT[g * K_PASS : (g + 1) * K_PASS, :].rearrange("(p j) c -> p (j c)", j=PACK)
+            nc.sync.dma_start(out=x_raw[n][:], in_=rows[:, j0 * T : (j0 + planes) * T])
             if n == 0:
                 nc.sync.dma_start(offs_sb[:], offs)
         w_raw = []
         for n, (g, a, b) in enumerate(W_LOADS):
-            w_raw.append(keep.tile([P, PACK, b - a], F32, name=f"w_raw{n}", tag=f"w_raw{n}", align_bytes=DMA_ALIGN))
+            w_raw.append(keep.tile([P, PACK, b - a], F32, name=f"w_raw{n}", align_bytes=DMA_ALIGN))
             rows = w1[g * K_PASS : (g + 1) * K_PASS, a:b]
             nc.sync.dma_start(out=w_raw[n][:], in_=rows.rearrange("(p j) c -> p j c", j=PACK))
         nc.sync.dma_start(pos_sb[:], pos1)
@@ -104,112 +95,105 @@ def tile_picked_mixup_gelu_e_kernel(
                 in_=w2_scales[0, SCALE_ROWS * q : SCALE_ROWS * (q + 1), :].bitcast(I32),
             )
 
-        x_words = [keep.tile([P, T], U32, name=f"x_words{g}", align_bytes=MX_ALIGN) for g in range(PASSES)]
-        picked_words = [keep.tile([P, S], U32, name=f"picked_words{g}", align_bytes=MX_ALIGN) for g in range(PASSES)]
-        picked_scales = keep.tile([P, S], U8, name="picked_scales", align_bytes=MX_ALIGN)
-        for n, (g, a, b, eighths) in enumerate(X_LOADS):
-            x_bf = keep.tile([P, b - a, PACK], BF16, name=f"x_bf{n}", align_bytes=MX_ALIGN)
-            share = (b - a) * eighths // 8
-            for move, c0, c1 in ((on_scalar, 0, share), (on_vector, share, b - a)):
-                if c1 > c0:
-                    move(
-                        x_bf[:, c0:c1, :].rearrange("p (c i) j -> p c j i", i=LINE),
-                        x_raw[n][:, :, c0:c1].rearrange("p j (c i) -> p c j i", i=LINE),
-                    )
-            nc.vector.quantize_mx(
-                out=x_words[g][:, a:b].bitcast(FP8X4),
-                scales=x_scales[SCALE_ROWS * g :, a:b],
-                in_=x_bf[:].rearrange("p c j -> p (c j)"),
-            )
-            if b == T:
-                if g == PASSES - 1:
-                    nc.vector.tensor_copy(out=picked_scales[:], in_=x_scales[:].indirect(offs_sb[:]))
-                nc.vector.tensor_copy(out=picked_words[g][:], in_=x_words[g][:].indirect(offs_sb[:]))
+        picked = [keep.tile([P, PACK, S], F32, name=f"picked{g}") for g in range(PASSES)]
+        x_codes = [keep.tile([P, S], U32, name=f"x_codes{g}", align_bytes=MX_ALIGN) for g in range(PASSES)]
+        x_scales = [keep.tile([P, S], U8, name=f"x_scales{g}", align_bytes=MX_ALIGN) for g in range(PASSES)]
 
-        for bank, width in (("b2", S), ("b3", S), ("b1", S // 2)):
-            warm = psum.tile([P, width], F32, name=f"warm_{bank}", tag=bank)
-            nc.tensor.matmul_mx(
-                out=warm[:],
-                lhsT=picked_words[0][:, :P].bitcast(FP8X4),
-                lhsT_scale=picked_scales[:, :P],
-                rhs=picked_words[0][:, :width].bitcast(FP8X4),
-                rhs_scale=picked_scales[:, :width],
-                start=True,
-                stop=True,
+        def gather(move, dst, window, entries, a, b):
+            move(dst[:, a:b], window.indirect(entries[:, a // LIST_ROWS : b // LIST_ROWS]))
+
+        def weave(move, dst, src, a, b):
+            move(
+                dst[:, a:b, :].rearrange("p (c i) j -> p c j i", i=LINE),
+                src[:, :, a:b].rearrange("p j (c i) -> p c j i", i=LINE),
             )
 
-        w_codes = {}
-        w_scales = keep.tile([P, H], U8, name="w_scales", align_bytes=MX_ALIGN)
-        w_scales_early = keep.tile([P, EARLY_TILES * P], U8, name="w_scales_early", align_bytes=MX_ALIGN)
+        def quantise_samples(g):
+            x_bf = keep.tile([P, S, PACK], BF16, name=f"x_bf{g}", align_bytes=MX_ALIGN)
+            weave(on_vector, x_bf, picked[g], HALF, S)
+            share = PIECE if g == 0 else PIECE // 2
+            weave(on_scalar, x_bf, picked[g], 0, share)
+            weave(on_vector, x_bf, picked[g], share, HALF)
+            for a in (HALF, 0):
+                nc.vector.quantize_mx(
+                    out=x_codes[g][:, a : a + HALF].bitcast(FP8X4),
+                    scales=x_scales[g][:, a : a + HALF],
+                    in_=x_bf[:, a : a + HALF, :].rearrange("p c j -> p (c j)"),
+                )
 
-        def w_scale_rows(g, cols):
-            if g == 0 and cols.stop <= EARLY_TILES * P:
-                return w_scales_early[:, cols]
-            return w_scales[SCALE_ROWS * g :, cols]
+        for n, (g, j0, planes) in enumerate(X_LOADS):
+            if n == len(X_LOADS) - 1:
+                gather(on_vector, picked[g][:, j0, :], x_raw[n][:], offs_sb, 0, HALF)
+                gather(on_scalar, picked[g][:, j0, :], x_raw[n][:], offs_sb, HALF, S)
+            else:
+                gather(on_scalar, picked[g][:, j0, :], x_raw[n][:], offs_sb, 0, S)
+                if planes == 2:
+                    gather(on_vector, picked[g][:, j0 + 1, :], x_raw[n][:, T:], offs_sb, 0, S)
+            if j0 + planes == PACK:
+                quantise_samples(g)
 
-        w_bf = {
-            (g, t0): keep.tile(
-                [P, EARLY_TILES, P, PACK], BF16, name=f"w_bf{g}{t0}", tag=f"w_bf{g}{t0}", align_bytes=MX_ALIGN
-            )
-            for g in range(PASSES)
-            for t0 in (0, EARLY_TILES)
-        }
+        w_bf = [keep.tile([P, PACK, P, PACK], BF16, name=f"w_bf{g}", align_bytes=MX_ALIGN) for g in range(PASSES)]
+        w_codes = [keep.tile([P, H], U32, name=f"w_codes{g}", align_bytes=MX_ALIGN) for g in range(PASSES)]
+        w_scale_tiles = [keep.tile([P, H], U8, name=f"w_scales{g}", align_bytes=MX_ALIGN) for g in range(PASSES)]
 
-        def on_gpsimd(dst, src):
-            nc.gpsimd.tensor_scalar(dst, src, 1.0, 0.0, MULT, ADD)
+        def w_scales(g, t):
+            if t == PACK - 1:
+                return w_scale_tiles[0][SCALE_ROWS * g :, t * P : (t + 1) * P]
+            return w_scale_tiles[g][:, t * P : (t + 1) * P]
 
-        def round_weights(move, n, t0):
+        def round_weights(move, n, t0, t1, c0=0, c1=None):
             g, a, b = W_LOADS[n]
-            dst = w_bf[g, t0][:, :, a // PACK : b // PACK, :]
-            src = w_raw[n][:].rearrange("p j (m t) -> p t m j", t=PACK)[:, t0 : t0 + EARLY_TILES, :, :]
-            if move != on_gpsimd:
-                dst, src = dst.rearrange("p t m j -> p m j t"), src.rearrange("p t m j -> p m j t")
-            move(dst, src)
-
-        for n, (g, a, b) in enumerate(W_LOADS):
-            round_weights(on_vector if b - a == P else on_scalar, n, 0)
-        for n, (g, a, b) in enumerate(W_LOADS):
-            round_weights(on_gpsimd if g == 0 else on_scalar, n, EARLY_TILES)
-
-        def quantise_weights(g, t0, t1):
-            cols = slice(t0 * P, t1 * P)
-            base = t0 // EARLY_TILES * EARLY_TILES
-            tag = "w_bf10" if g == 0 and t0 >= EARLY_TILES else f"w_codes{g}{t0}"
-            codes = keep.tile([P, (t1 - t0) * P], U32, name=f"w_codes{g}{t0}", tag=tag, align_bytes=MX_ALIGN)
-            for t in range(t0, t1):
-                w_codes[g, t] = codes[:, (t - t0) * P : (t - t0 + 1) * P]
-            nc.vector.quantize_mx(
-                out=codes[:].bitcast(FP8X4),
-                scales=w_scale_rows(g, cols),
-                in_=w_bf[g, base][:, t0 - base : t1 - base, :, :].rearrange("p t m j -> p (t m j)"),
+            c1 = b - a if c1 is None else c1
+            move(
+                w_bf[g][:, t0:t1, (a + c0) // PACK : (a + c1) // PACK, :].rearrange("p t m j -> p m j t"),
+                w_raw[n][:, :, c0:c1].rearrange("p j (m t) -> p m j t", t=PACK)[:, :, :, t0:t1],
             )
 
-        for g in range(PASSES):
-            for t in range(EARLY_TILES):
-                quantise_weights(g, t, t + 1)
-        for g in range(PASSES):
-            quantise_weights(g, EARLY_TILES, PACK)
+        def quantise_weights(g):
+            for t in range(PACK):
+                cols = slice(t * P, (t + 1) * P)
+                nc.vector.quantize_mx(
+                    out=w_codes[g][:, cols].bitcast(FP8X4),
+                    scales=w_scales(g, t),
+                    in_=w_bf[g][:, t, :, :].rearrange("p m j -> p (m j)"),
+                )
 
-        for t in range(PACK):
-            cols = slice(t * P, (t + 1) * P)
-            parts = (("a0", 0, S // 2), ("b0", S // 2, S)) if t == 0 else ((f"a{t}", 0, S),)
-            for bank, a, b in parts:
-                u = psum.tile([P, b - a], F32, name=f"u{t}{bank}", tag=bank)
-                for g in range(PASSES):
-                    nc.tensor.matmul_mx(
-                        out=u[:],
-                        lhsT=w_codes[g, t].bitcast(FP8X4),
-                        lhsT_scale=w_scale_rows(g, cols),
-                        rhs=picked_words[g][:, a:b].bitcast(FP8X4),
-                        rhs_scale=picked_scales[SCALE_ROWS * g :, a:b],
-                        start=(g == 0),
-                        stop=(g == PASSES - 1),
-                    )
-                nc.scalar.activation(out=h[t][:, a:b], in_=u[:], func=GELU)
+        round_weights(on_scalar, 0, 0, PACK)
+        round_weights(on_vector, 1, 0, PACK, 0, P)
+        round_weights(on_scalar, 1, 0, PACK, P, 2 * P)
+        quantise_weights(0)
+        round_weights(on_scalar, 2, 0, PACK)
+        round_weights(on_vector, 3, 0, PACK)
+        round_weights(on_vector, 4, 0, PACK // 2)
+        round_weights(on_scalar, 4, PACK // 2, PACK)
+        quantise_weights(1)
+
+        parts = [(0, "a0", 0, HALF), (0, "b0", HALF, S)] + [(t, f"a{t}", 0, S) for t in range(1, PACK)]
+        u = {bank: psum.tile([P, b - a], F32, name=f"u{bank}", tag=bank) for t, bank, a, b in parts}
+        for g in range(PASSES):
+            for t, bank, a, b in parts:
+                cols = slice(t * P, (t + 1) * P)
+                nc.tensor.matmul_mx(
+                    out=u[bank][:],
+                    lhsT=w_codes[g][:, cols].bitcast(FP8X4),
+                    lhsT_scale=w_scales(g, t),
+                    rhs=x_codes[g][:, a:b].bitcast(FP8X4),
+                    rhs_scale=x_scales[g][:, a:b],
+                    start=(g == 0),
+                    stop=(g == PASSES - 1),
+                )
+        for t, bank, a, b in parts:
+            nc.scalar.activation(out=h[t][:, a:b], in_=u[bank][:], func=GELU)
 
         partner = keep.tile([P, PACK, S], F32, name="partner")
+        fetched = keep.tile([P, S], F32, name="fetched")
+        on_scalar(fetched[:], h[SCALAR_TILE][:].indirect(pos_sb[:]))
         for t in range(PACK):
-            nc.vector.tensor_tensor(partner[:, t, :], h[t][:].indirect(pos_sb[:]), mu_sb[:], MULT)
+            if t != SCALAR_TILE:
+                nc.vector.tensor_tensor(partner[:, t, :], h[t][:].indirect(pos_sb[:]), mu_sb[:], MULT)
+        for a in (0, HALF):
+            cols = slice(a, a + HALF)
+            nc.vector.tensor_tensor(partner[:, SCALAR_TILE, cols], fetched[:, cols], mu_sb[:, cols], MULT)
 
         own = {}
         scaled = {}

@@ -34,7 +34,8 @@ PIECE = 128
 PIECES = S // PIECE
 HALF = S // 2
 H_COLS = S + 16
-SCALAR_TILE = 2
+SCALAR_TILE = PACK - 1
+TILE_ORDER = (0, 1, SCALAR_TILE, 2)
 
 
 def tile_picked_mixup_gelu_e_kernel(
@@ -137,7 +138,7 @@ def tile_picked_mixup_gelu_e_kernel(
         w_scale_tiles = [keep.tile([P, H], U8, name=f"w_scales{g}", align_bytes=MX_ALIGN) for g in range(PASSES)]
 
         def w_scales(g, t):
-            if t == PACK - 1:
+            if t == TILE_ORDER[-1]:
                 return w_scale_tiles[0][SCALE_ROWS * g :, t * P : (t + 1) * P]
             return w_scale_tiles[g][:, t * P : (t + 1) * P]
 
@@ -150,7 +151,7 @@ def tile_picked_mixup_gelu_e_kernel(
             )
 
         def quantise_weights(g):
-            for t in range(PACK):
+            for t in TILE_ORDER:
                 cols = slice(t * P, (t + 1) * P)
                 nc.vector.quantize_mx(
                     out=w_codes[g][:, cols].bitcast(FP8X4),
@@ -162,13 +163,14 @@ def tile_picked_mixup_gelu_e_kernel(
         round_weights(on_vector, 1, 0, PACK, 0, P)
         round_weights(on_scalar, 1, 0, PACK, P, 2 * P)
         quantise_weights(0)
-        round_weights(on_scalar, 2, 0, PACK)
+        round_weights(on_scalar, 2, 0, PACK, 0, 3 * P // 2)
+        round_weights(on_vector, 2, 0, PACK, 3 * P // 2, 2 * P)
         round_weights(on_vector, 3, 0, PACK)
-        round_weights(on_vector, 4, 0, PACK // 2)
-        round_weights(on_scalar, 4, PACK // 2, PACK)
+        round_weights(on_scalar, 4, 0, 1)
+        round_weights(on_vector, 4, 1, PACK)
         quantise_weights(1)
 
-        parts = [(0, "a0", 0, HALF), (0, "b0", HALF, S)] + [(t, f"a{t}", 0, S) for t in range(1, PACK)]
+        parts = [(0, "a0", 0, HALF), (0, "b0", HALF, S)] + [(t, f"a{t}", 0, S) for t in TILE_ORDER[1:]]
         u = {bank: psum.tile([P, b - a], F32, name=f"u{bank}", tag=bank) for t, bank, a, b in parts}
         for g in range(PASSES):
             for t, bank, a, b in parts:
@@ -185,15 +187,15 @@ def tile_picked_mixup_gelu_e_kernel(
         for t, bank, a, b in parts:
             nc.scalar.activation(out=h[t][:, a:b], in_=u[bank][:], func=GELU)
 
-        partner = keep.tile([P, PACK, S], F32, name="partner")
-        fetched = keep.tile([P, S], F32, name="fetched")
-        on_scalar(fetched[:], h[SCALAR_TILE][:].indirect(pos_sb[:]))
+        partner_row = keep.tile([P, PACK * S + HALF], F32, name="partner_row")
+        partner = partner_row[:, : PACK * S].rearrange("p (t c) -> p t c", t=PACK)
+        fetched = partner_row[:, PACK * S - HALF :]
+        on_scalar(fetched, h[SCALAR_TILE][:].indirect(pos_sb[:]))
         for t in range(PACK):
             if t != SCALAR_TILE:
                 nc.vector.tensor_tensor(partner[:, t, :], h[t][:].indirect(pos_sb[:]), mu_sb[:], MULT)
-        for a in (0, HALF):
-            cols = slice(a, a + HALF)
-            nc.vector.tensor_tensor(partner[:, SCALAR_TILE, cols], fetched[:, cols], mu_sb[:, cols], MULT)
+        for engine, a, b in ((nc.vector, 0, PIECE), (nc.vector, PIECE, HALF), (nc.gpsimd, HALF, S)):
+            engine.tensor_tensor(partner[:, SCALAR_TILE, a:b], fetched[:, a:b], mu_sb[:, a:b], MULT)
 
         own = {}
         scaled = {}
@@ -208,7 +210,11 @@ def tile_picked_mixup_gelu_e_kernel(
             for t in range(PACK):
                 nc.tensor.transpose(turned[:, t, :], h[t][:, n * PIECE : (n + 1) * PIECE], ident[:])
             scaled[n] = keep.tile([P, PACK, P], F32, name=f"scaled{n}")
-            nc.scalar.activation(out=scaled[n][:], in_=turned[:], func=COPY, scale=lam_col[:, n : n + 1])
+            for t0 in (0, PACK // 2):
+                pair = slice(t0, t0 + PACK // 2)
+                nc.scalar.activation(
+                    out=scaled[n][:, pair, :], in_=turned[:, pair, :], func=COPY, scale=lam_col[:, n : n + 1]
+                )
             if n > 0:
                 turn_back(n - 1)
         turn_back(PIECES - 1)

from contextlib import ExitStack

import concourse.mybir as mybir
from concourse.masks import make_identity

K, T, S, H, N = 1024, 1024, 512, 512, 256
FLOPS = 2 * K * H * S + 2 * H * N * S

F32 = mybir.dt.float32
BF16 = mybir.dt.bfloat16
I32 = mybir.dt.int32
U32 = mybir.dt.uint32
U16 = mybir.dt.uint16
U8 = mybir.dt.uint8
FP8X4 = mybir.dt.float8_e4m3fn_x4
COPY = mybir.ActivationFunctionType.Copy
GELU = mybir.ActivationFunctionType.Gelu_apprx_tanh
MULT = mybir.AluOpType.mult
ADD = mybir.AluOpType.add

P = 128
PACK = 4
K_PASS = P * PACK
PASSES = K // K_PASS
SCALE_ROWS = 4
LINE = 4
LIST_ROWS = 16
MX_ALIGN = 64
DMA_ALIGN = 256

X_LOADS = ((0, 0, 2), (0, 2, 2), (1, 0, 2), (1, 2, 1), (1, 3, 1))
W_LOADS = ((0, 0, H // 2), (0, H // 2, H), (1, 0, H // 2), (1, H // 2, H - P), (1, H - P, H))
PIECE = 128
PIECES = S // PIECE
HALF = S // 2
H_COLS = S + 16
SCALAR_TILE = PACK - 1
TILE_ORDER = (0, 1, SCALAR_TILE, 2)


def tile_picked_mixup_gelu_e_kernel(
    tc, xT, w1, w2_words, w2_scales, lam, mu, offs, pos1, out
):
    nc = tc.nc

    def on_vector(dst, src):
        nc.vector.tensor_copy(out=dst, in_=src)

    def on_scalar(dst, src):
        nc.scalar.activation(out=dst, in_=src, func=COPY)

    with ExitStack() as ctx:
        keep = ctx.enter_context(tc.tile_pool(name="keep", bufs=1))
        psum = ctx.enter_context(tc.psum_pool(name="psum", bufs=1))

        offs_sb = keep.tile([P, S // LIST_ROWS], U16, name="offs_sb")
        pos_sb = keep.tile([P, S // LIST_ROWS], U16, name="pos_sb")

        w2_scale_sb = keep.tile([P, N], U8, name="w2_scale_sb", align_bytes=MX_ALIGN)
        nc.gpsimd.memset(w2_scale_sb[:], 0)

        ident = keep.tile([P, P], F32, name="ident")
        make_identity(nc, ident[:])

        h = [keep.tile([P, H_COLS], F32, name=f"h{t}") for t in range(PACK)]
        zero = keep.tile([P, H_COLS - S], F32, name="zero")
        nc.vector.memset(zero[:], 0.0)
        for t in range(PACK):
            nc.scalar.activation(out=h[t][:, S:], in_=zero[:], func=GELU)

        x_raw = []
        for n, (g, j0, planes) in enumerate(X_LOADS):
            x_raw.append(keep.tile([P, planes * T], F32, name=f"x_raw{n}", align_bytes=DMA_ALIGN))
            rows = xT[g * K_PASS : (g + 1) * K_PASS, :].rearrange("(p j) c -> p (j c)", j=PACK)
            nc.sync.dma_start(out=x_raw[n][:], in_=rows[:, j0 * T : (j0 + planes) * T])
            if n == 0:
                nc.sync.dma_start(offs_sb[:], offs)
        w_raw = []
        for n, (g, a, b) in enumerate(W_LOADS):
            w_raw.append(keep.tile([P, PACK, b - a], F32, name=f"w_raw{n}", align_bytes=DMA_ALIGN))
            rows = w1[g * K_PASS : (g + 1) * K_PASS, a:b]
            nc.sync.dma_start(out=w_raw[n][:], in_=rows.rearrange("(p j) c -> p j c", j=PACK))
        nc.sync.dma_start(pos_sb[:], pos1)
        mu_sb = keep.tile([P, S], F32, name="mu_sb", align_bytes=DMA_ALIGN)
        nc.sync.dma_start(out=mu_sb[:], in_=mu)
        lam_col = keep.tile([P, PIECES], F32, name="lam_col")
        with nc.allow_non_contiguous_dma(reason="one share to a partition"):
            nc.sync.dma_start(out=lam_col[:], in_=lam[0, :].rearrange("(n p) -> p n", p=PIECE))
        w2_codes = keep.tile([P, N], U32, name="w2_codes", align_bytes=DMA_ALIGN)
        nc.sync.dma_start(
            out=w2_codes[:].bitcast(I32), in_=w2_words[0].rearrange("p n t -> p (n t)").bitcast(I32)
        )
        for q in range(P // 32):
            nc.sync.dma_start(
                out=w2_scale_sb[32 * q : 32 * q + SCALE_ROWS, :].bitcast(I32),
                in_=w2_scales[0, SCALE_ROWS * q : SCALE_ROWS * (q + 1), :].bitcast(I32),
            )

        picked = [keep.tile([P, PACK, S], F32, name=f"picked{g}") for g in range(PASSES)]
        x_codes = [keep.tile([P, S], U32, name=f"x_codes{g}", align_bytes=MX_ALIGN) for g in range(PASSES)]
        x_scales = [keep.tile([P, S], U8, name=f"x_scales{g}", align_bytes=MX_ALIGN) for g in range(PASSES)]

        def gather(move, dst, window, entries, a, b):
            move(dst[:, a:b], window.indirect(entries[:, a // LIST_ROWS : b // LIST_ROWS]))

        def weave(move, dst, src, a, b):
            move(
                dst[:, a:b, :].rearrange("p (c i) j -> p c j i", i=LINE),
                src[:, :, a:b].rearrange("p j (c i) -> p c j i", i=LINE),
            )

        def quantise_samples(g):
            x_bf = keep.tile([P, S, PACK], BF16, name=f"x_bf{g}", align_bytes=MX_ALIGN)
            weave(on_vector, x_bf, picked[g], HALF, S)
            share = PIECE if g == 0 else PIECE // 2
            weave(on_scalar, x_bf, picked[g], 0, share)
            weave(on_vector, x_bf, picked[g], share, HALF)
            for a in (HALF, 0):
                nc.vector.quantize_mx(
                    out=x_codes[g][:, a : a + HALF].bitcast(FP8X4),
                    scales=x_scales[g][:, a : a + HALF],
                    in_=x_bf[:, a : a + HALF, :].rearrange("p c j -> p (c j)"),
                )

        for n, (g, j0, planes) in enumerate(X_LOADS):
            if n == len(X_LOADS) - 1:
                gather(on_vector, picked[g][:, j0, :], x_raw[n][:], offs_sb, 0, HALF)
                gather(on_scalar, picked[g][:, j0, :], x_raw[n][:], offs_sb, HALF, S)
            else:
                gather(on_scalar, picked[g][:, j0, :], x_raw[n][:], offs_sb, 0, S)
                if planes == 2:
                    gather(on_vector, picked[g][:, j0 + 1, :], x_raw[n][:, T:], offs_sb, 0, S)
            if j0 + planes == PACK:
                quantise_samples(g)

        w_bf = [keep.tile([P, PACK, P, PACK], BF16, name=f"w_bf{g}", align_bytes=MX_ALIGN) for g in range(PASSES)]
        w_codes = [keep.tile([P, H], U32, name=f"w_codes{g}", align_bytes=MX_ALIGN) for g in range(PASSES)]
        w_scale_tiles = [keep.tile([P, H], U8, name=f"w_scales{g}", align_bytes=MX_ALIGN) for g in range(PASSES)]

        def w_scales(g, t):
            if t == TILE_ORDER[-1]:
                return w_scale_tiles[0][SCALE_ROWS * g :, t * P : (t + 1) * P]
            return w_scale_tiles[g][:, t * P : (t + 1) * P]

        def round_weights(move, n, t0, t1, c0=0, c1=None):
            g, a, b = W_LOADS[n]
            c1 = b - a if c1 is None else c1
            move(
                w_bf[g][:, t0:t1, (a + c0) // PACK : (a + c1) // PACK, :].rearrange("p t m j -> p m j t"),
                w_raw[n][:, :, c0:c1].rearrange("p j (m t) -> p m j t", t=PACK)[:, :, :, t0:t1],
            )

        def quantise_weights(g):
            for t in TILE_ORDER:
                cols = slice(t * P, (t + 1) * P)
                nc.vector.quantize_mx(
                    out=w_codes[g][:, cols].bitcast(FP8X4),
                    scales=w_scales(g, t),
                    in_=w_bf[g][:, t, :, :].rearrange("p m j -> p (m j)"),
                )

        round_weights(on_scalar, 0, 0, PACK)
        round_weights(on_vector, 1, 0, PACK, 0, P)
        round_weights(on_scalar, 1, 0, PACK, P, 2 * P)
        quantise_weights(0)
        round_weights(on_scalar, 2, 0, PACK, 0, 3 * P // 2)
        round_weights(on_vector, 2, 0, PACK, 3 * P // 2, 2 * P)
        round_weights(on_vector, 3, 0, PACK)
        round_weights(on_scalar, 4, 0, 1)
        round_weights(on_vector, 4, 1, PACK)
        quantise_weights(1)

        parts = [(0, "a0", 0, HALF), (0, "b0", HALF, S)] + [(t, f"a{t}", 0, S) for t in TILE_ORDER[1:]]
        u = {bank: psum.tile([P, b - a], F32, name=f"u{bank}", tag=bank) for t, bank, a, b in parts}
        for g in range(PASSES):
            for t, bank, a, b in parts:
                cols = slice(t * P, (t + 1) * P)
                nc.tensor.matmul_mx(
                    out=u[bank][:],
                    lhsT=w_codes[g][:, cols].bitcast(FP8X4),
                    lhsT_scale=w_scales(g, t),
                    rhs=x_codes[g][:, a:b].bitcast(FP8X4),
                    rhs_scale=x_scales[g][:, a:b],
                    start=(g == 0),
                    stop=(g == PASSES - 1),
                )
        for t, bank, a, b in parts:
            nc.scalar.activation(out=h[t][:, a:b], in_=u[bank][:], func=GELU)

        partner_row = keep.tile([P, PACK * S + HALF], F32, name="partner_row")
        partner = partner_row[:, : PACK * S].rearrange("p (t c) -> p t c", t=PACK)
        fetched = partner_row[:, PACK * S - HALF :]
        on_scalar(fetched, h[SCALAR_TILE][:].indirect(pos_sb[:]))
        for t in range(PACK):
            if t != SCALAR_TILE:
                nc.vector.tensor_tensor(partner[:, t, :], h[t][:].indirect(pos_sb[:]), mu_sb[:], MULT)
        for engine, a, b in ((nc.vector, 0, PIECE), (nc.vector, PIECE, HALF), (nc.gpsimd, HALF, S)):
            engine.tensor_tensor(partner[:, SCALAR_TILE, a:b], fetched[:, a:b], mu_sb[:, a:b], MULT)

        own = {}
        scaled = {}

        def turn_back(n):
            own[n] = psum.tile([P, PACK, PIECE], F32, name=f"own{n}", tag=f"a{n}")
            for t in range(PACK):
                nc.tensor.transpose(own[n][:, t, :], scaled[n][:, t, :], ident[:])

        for n in range(PIECES):
            turned = psum.tile([P, PACK, P], F32, name=f"turned{n}", tag=f"b{n}")
            for t in range(PACK):
                nc.tensor.transpose(turned[:, t, :], h[t][:, n * PIECE : (n + 1) * PIECE], ident[:])
            scaled[n] = keep.tile([P, PACK, P], F32, name=f"scaled{n}")
            for t0 in (0, PACK // 2):
                pair = slice(t0, t0 + PACK // 2)
                nc.scalar.activation(
                    out=scaled[n][:, pair, :], in_=turned[:, pair, :], func=COPY, scale=lam_col[:, n : n + 1]
                )
            if n > 0:
                turn_back(n - 1)
        turn_back(PIECES - 1)

        out_view = out.rearrange("(r p) j -> p r j", p=P)
        z_bf = [keep.tile([P, PIECE, PACK], BF16, name=f"z_bf{n}", align_bytes=MX_ALIGN) for n in range(PIECES)]

        y_sb = keep.tile([P, N // P, S], F32, name="y_sb", align_bytes=DMA_ALIGN)

        def mix(n):
            cols = slice(n * PIECE, (n + 1) * PIECE)
            nc.vector.tensor_tensor(
                z_bf[n][:].rearrange("p (c i) t -> p c t i", i=LINE),
                own[n][:].rearrange("p t (c i) -> p c t i", i=LINE),
                partner[:, :, cols].rearrange("p t (c i) -> p c t i", i=LINE),
                ADD,
            )

        def second_product(n):
            cols = slice(n * PIECE, (n + 1) * PIECE)
            z_codes = keep.tile([P, PIECE], U32, name=f"z_codes{n}", align_bytes=MX_ALIGN)
            z_scales = keep.tile([P, PIECE], U8, name=f"z_scales{n}", align_bytes=MX_ALIGN)
            nc.vector.quantize_mx(
                out=z_codes[:].bitcast(FP8X4), scales=z_scales[:], in_=z_bf[n][:].rearrange("p c t -> p (c t)")
            )
            last = n == PIECES - 1
            y = [psum.tile([P, N // P, PIECE], F32, name=f"y{n}", tag=f"b{PIECES - 1 - n}")] * 2
            if last:
                y[1] = psum.tile([P, N // P, PIECE], F32, name="y_second", tag="a0")
            for r in range(N // P):
                rows = slice(r * P, (r + 1) * P)
                nc.tensor.matmul_mx(
                    out=y[r][:, r, :],
                    lhsT=w2_codes[:, rows].bitcast(FP8X4),
                    lhsT_scale=w2_scale_sb[:, rows],
                    rhs=z_codes[:].bitcast(FP8X4),
                    rhs_scale=z_scales[:],
                    start=True,
                    stop=True,
                )
            if last:
                for r, copy in enumerate((nc.scalar.copy, nc.vector.tensor_copy)):
                    copy(out=y_sb[:, r, cols], in_=y[r][:, r, :])
            else:
                nc.scalar.copy(out=y_sb[:, :, cols], in_=y[0][:])
            if n > 0:
                stored = slice(0 if n == 1 else cols.start, cols.stop)
                nc.sync.dma_start(out=out_view[:, :, stored], in_=y_sb[:, :, stored])

        for n in range(PIECES + 1):
            if n < PIECES:
                mix(n)
            if n > 0:
                second_product(n - 1)
